import numpy as np
import ml_dtypes


def mxq(x, axis, fmt="e4m3"):
    dtype, down = {"e4m3": (ml_dtypes.float8_e4m3fn, 7), "e5m2": (ml_dtypes.float8_e5m2, 14)}[fmt]
    v = np.moveaxis(np.asarray(x, np.float32).astype(ml_dtypes.bfloat16).astype(np.float64), axis, -1)
    blocks = v.reshape(v.shape[:-1] + (-1, 32))
    amax = np.abs(blocks).max(-1, keepdims=True)
    byte = np.maximum(np.where(amax > 0, np.frexp(amax)[1] - 1 + 127, 0) - down, 1)
    scale = np.exp2(byte - 127.0)
    codes = (blocks / scale).astype(np.float32).astype(dtype).astype(np.float64)
    return np.moveaxis((codes * scale).reshape(v.shape), -1, axis)


WIDE = False


def mx_kscale(k):
    if not WIDE:
        return np.ones(k)
    levels = np.array([10, -10, 5, -5, 0])
    if k % 512:
        return np.exp2(np.random.permutation(np.resize(levels, k // 32))).repeat(32)
    a = np.empty((k // 512, 16))
    for p in range(k // 512):
        a[p, :8] = np.random.permutation(np.resize(levels, 8))
        for g in range(8):
            far = levels[np.abs(levels - a[p, g]) >= 10]
            a[p, g + 8] = far[np.random.randint(len(far))]
    return np.exp2(a.ravel()).repeat(32)


def f64(x):
    return np.asarray(x).astype(np.float64)


def striped(idx):
    return np.tile(idx.reshape(-1, 16).T, (8, 1)).astype(np.uint16)


def unstriped(offs):
    return offs[:16].T.reshape(-1).astype(np.int64)


E2M1 = np.array([0.0, 0.5, 1.0, 1.5, 2.0, 3.0, 4.0, 6.0, -0.0, -0.5, -1.0, -1.5, -2.0, -3.0, -4.0, -6.0])


def pack_weight(w, fmt):
    k, n = w.shape
    w = f64(np.asarray(w, np.float32).astype(ml_dtypes.bfloat16)).reshape(k // 32, 32, n)
    amax = np.abs(w).max(1)
    if fmt == "e4m3":
        byte = np.frexp(amax)[1] - 1 + 127 - 7
    else:
        mant, ex = np.frexp(amax / 6.0)
        byte = np.where(mant > 0.5, ex, ex - 1) + 127
    byte = np.clip(np.where(amax > 0, byte, 1), 1, 254)
    scaled = (w * np.exp2(127.0 - byte)[:, None, :]).reshape(k, n).astype(np.float32)
    by_word = np.ascontiguousarray(scaled.reshape(k // 512, 128, 4, n).transpose(0, 1, 3, 2))
    if fmt == "e4m3":
        words = by_word.astype(ml_dtypes.float8_e4m3fn).view(np.uint8)
    else:
        c = by_word.astype(ml_dtypes.float4_e2m1fn).view(np.uint8) & 0xF
        words = (c[..., 0::2] | (c[..., 1::2] << 4)).reshape(k // 512, 128, 2 * n)
    return np.ascontiguousarray(words), np.ascontiguousarray(byte.astype(np.uint8).reshape(k // 512, 16, n))


def unpack_weight(words, scales, fmt):
    g, _, n = scales.shape
    words = np.ascontiguousarray(words).reshape(g, 128, n, -1)
    if fmt == "e4m3":
        vals = words.view(ml_dtypes.float8_e4m3fn).astype(np.float64)
    else:
        nib = np.empty((g, 128, n, 4), np.uint8)
        nib[..., 0::2] = words & 0xF
        nib[..., 1::2] = words >> 4
        vals = E2M1[nib]
    vals = vals * np.repeat(np.exp2(scales.astype(np.float64) - 127.0), 8, axis=1)[..., None]
    return vals.transpose(0, 1, 3, 2).reshape(g * 512, n)


def gelu(v):
    return 0.5 * v * (1.0 + np.tanh(np.sqrt(2.0 / np.pi) * (v + 0.044715 * v**3)))


K, T, K2, TB, S, H, T2, P, N = 1024, 2048, 512, 1024, 512, 1024, 2048, 1024, 512

def setup_inputs():
    n = np.random.standard_normal
    s, s2, u = mx_kscale(K)[:, None], mx_kscale(K2)[:, None], mx_kscale(H)[:, None]
    d = {}
    d["tab_words"], d["tab_scales"] = pack_weight(n((K, T)) * s, "e4m3")
    d["tab2_words"], d["tab2_scales"] = pack_weight(n((K2, TB)) * s2, "e4m3")
    d["offs"] = striped(np.random.permutation(T)[:S])
    d["offs2"] = striped(np.random.permutation(TB)[:S])
    perm = np.random.permutation(T2)
    d["offs3"] = striped(perm[:S])
    d["offs4"] = striped(perm[S:2 * S])
    d["offs5"] = striped(np.random.permutation(T2)[:P])
    d["w1"] = (1.5 * n((K, H)) / K ** 0.5 / s).astype(np.float32)
    d["w2_words"], d["w2_scales"] = pack_weight(n((K2, H)) / K2 ** 0.5 / s2, "e2m1")
    d["w3"] = (1.2 * n((K2, H)) / K2 ** 0.5 / s2).astype(np.float32)
    d["wg1"] = np.exp(0.3 * n((128, S))).astype(np.float32)
    d["wg2"] = np.exp(0.3 * n((128, S))).astype(np.float32)
    d["page0"] = (1.2 * n((H, T2))).astype(np.float32)
    d["gain"] = (np.exp(0.4 * n(H)) * u[:, 0]).astype(np.float32)
    d["w4_words"], d["w4_scales"] = pack_weight(1.3 * n((H, N)) / H ** 0.5 / u, "e2m1")
    d["w5"] = (1.3 * n((H, N)) / H ** 0.5 / u).astype(np.float32)
    return d

def reference(tab_words, tab_scales, tab2_words, tab2_scales, offs, offs2, offs3, offs4, offs5,
              w1, w2_words, w2_scales, w3, wg1, wg2, page0, gain, w4_words, w4_scales, w5):
    v = unpack_weight(tab_words, tab_scales, "e4m3")[:, unstriped(offs)]
    v2 = unpack_weight(tab2_words, tab2_scales, "e4m3")[:, unstriped(offs2)]
    b = mxq(f64(w1), 0, "e4m3").T @ v
    h1 = 0.5 * b * (1.0 + np.tanh(0.7978845608 * (b + 0.044715 * b ** 3)))
    base = unpack_weight(w2_words, w2_scales, "e2m1").T @ v2
    h2 = base - np.abs(mxq(f64(w3), 0, "e4m3").T @ v2)
    page = f64(page0).copy()
    page[:, unstriped(offs3)] = np.tile(f64(wg1), (H // 128, 1)) * h1
    page[:, unstriped(offs4)] = np.tile(f64(wg2), (H // 128, 1)) * h2
    x = np.tanh(page[:, unstriped(offs5)]) * f64(gain)[:, None]
    xq = mxq(x, 0, "e4m3")
    y1 = unpack_weight(w4_words, w4_scales, "e2m1").T @ xq
    y2 = mxq(f64(w5), 0, "e4m3").T @ xq
    return np.abs(y1 - np.abs(y2))

@@ -1,0 +1,396 @@
+from contextlib import ExitStack
+
+import concourse.mybir as mybir
+from concourse.masks import make_identity
+
+K, T, K2, TB, S, H, T2, NP, N = 1024, 2048, 512, 1024, 512, 1024, 2048, 1024, 512
+FLOPS = 2 * S * H * (K + 2 * K2) + 2 * 2 * H * N * NP
+
+F32 = mybir.dt.float32
+BF16 = mybir.dt.bfloat16
+I32 = mybir.dt.int32
+U32 = mybir.dt.uint32
+U16 = mybir.dt.uint16
+U8 = mybir.dt.uint8
+FP8X4 = mybir.dt.float8_e4m3fn_x4
+FP4X4 = mybir.dt.float4_e2m1fn_x4
+ACT = mybir.ActivationFunctionType
+ALU = mybir.AluOpType
+
+P = 128
+PACK = 4
+KP = P * PACK
+CH = 256
+NCH = NP // CH
+ROUND_ON_VECTOR = (0, 1, 2, 3)
+ABS_ON_VECTOR = 3
+PAGE_SLOT = ["slot%d" % i for i in range(8)]
+
+
+def tile_list_crock_slot_scores_kernel(
+    tc, tab_words, tab_scales, tab2_words, tab2_scales, offs, offs2, offs3, offs4, offs5,
+    w1, w2_words, w2_scales, w3, wg1, wg2, page0, gain, w4_words, w4_scales, w5, out,
+):
+    nc = tc.nc
+    with ExitStack() as ctx:
+        lists = ctx.enter_context(tc.tile_pool(name="lists", bufs=1))
+        keep = ctx.enter_context(tc.tile_pool(name="keep", bufs=1))
+        ring = ctx.enter_context(tc.tile_pool(name="ring", bufs=1))
+        psum = ctx.enter_context(tc.psum_pool(name="psum", bufs=1))
+
+        def kept(name, shape, dtype):
+            return keep.tile(shape, dtype, name=name, align_bytes=64)
+
+        def load_list(name, src):
+            tile = lists.tile(list(src.shape), U16, name=name)
+            nc.sync.dma_start(tile[:], src)
+            return tile
+
+        def raw_tile(name, shape, dtype):
+            return ring.tile(shape, dtype, name=name, tag="raw", bufs=5, align_bytes=64)
+
+        def bank(name, index, shape):
+            return psum.tile(shape, F32, name=name, tag="bank%d" % index)
+
+        t2_scales = kept("t2_scales", [P, TB], U8)
+        w2_sc_raw = kept("w2_sc_raw", [P, H], U8)
+        t_scales = kept("t_scales", [P, T], U8)
+        w4_sc = kept("w4_sc", [P, 2, N], U8)
+        nc.vector.memset(t2_scales[:].bitcast(I32), 0)
+        nc.vector.memset(w2_sc_raw[:].bitcast(I32), 0)
+        nc.vector.memset(t_scales[:].bitcast(I32), 0)
+        nc.vector.memset(w4_sc[:].bitcast(I32), 0)
+
+        t2_words = kept("t2_words", [P, TB], U32)
+        nc.sync.dma_start(t2_words[:].bitcast(I32), tab2_words[0].rearrange("p n i -> p (n i)").bitcast(I32))
+        idx2 = load_list("idx2", offs2)
+
+        def load_rows(name, w, a, c0, width):
+            raw = raw_tile(name, [P, PACK, width], F32)
+            nc.sync.dma_start(raw[:], w[KP * a : KP * (a + 1), c0 : c0 + width].rearrange("(p j) c -> p j c", j=PACK))
+            return raw
+
+        identity = kept("identity", [P, P], F32)
+        make_identity(nc, identity[:])
+
+        def turn_gate(name, rows):
+            turned = bank(name + "_turned", 4, [P, PACK, P])
+            for jt in range(PACK):
+                nc.tensor.transpose(turned[:, jt, :], rows[:, P * jt : P * (jt + 1)], identity[:])
+            return turned
+
+        def deal_gate(name, turned, t):
+            spread = keep.tile([P, PACK, 4, 32], F32, name="%s_spread%d" % (name, t), tag="spread%d" % (t % 2))
+            nc.scalar.copy(
+                out=spread[:],
+                in_=turned[:].rearrange("p jt (q t) -> p jt q t", t=PACK)[:, :, :, t].unsqueeze(2).broadcast_to([P, PACK, 4, 32]),
+            )
+            back = bank("%s_back%d" % (name, t), 5 + t % 2, [P, S])
+            for jt in range(PACK):
+                nc.tensor.transpose(back[:, P * jt : P * (jt + 1)], spread[:, jt, :, :].rearrange("p r q -> p (r q)"), identity[:])
+            dealt = kept("%s_%d" % (name, t), [P, S], F32)
+            nc.scalar.copy(out=dealt[:], in_=back[:])
+            return dealt[:]
+
+        pages = {}
+
+        def load_page(i):
+            b, t = divmod(i, PACK)
+            pages[i] = keep.tile([P, T2], F32, name="page%d" % i, tag=PAGE_SLOT[i], align_bytes=64)
+            nc.sync.dma_start(pages[i][:], page0[KP * b : KP * (b + 1), :].rearrange("(p t) c -> t p c", t=PACK)[t])
+
+        w3_head = [load_rows("w3_head0", w3, 0, 0, KP // 2)]
+        for q in range(4):
+            nc.sync.dma_start(t2_scales[32 * q : 32 * q + 4, :].bitcast(I32), tab2_scales[0, 4 * q : 4 * q + 4, :].bitcast(I32))
+        w3_head.append(load_rows("w3_head1", w3, 0, KP // 2, KP // 2))
+        wg2_rows = keep.tile([P, S], F32, name="wg2_rows", tag="h1_0", align_bytes=64)
+        nc.sync.dma_start(wg2_rows[:], wg2)
+        w2_raw = kept("w2_raw", [P, 2 * H], U8)
+        nc.sync.dma_start(w2_raw[:].bitcast(I32), w2_words[0].bitcast(I32))
+        for q in range(4):
+            nc.sync.dma_start(w2_sc_raw[32 * q : 32 * q + 4, :].bitcast(I32), w2_scales[0, 4 * q : 4 * q + 4, :].bitcast(I32))
+        idx4 = load_list("idx4", offs4)
+        load_page(0)
+        load_page(1)
+        wg1_rows = keep.tile([P, S], F32, name="wg1_rows", tag="h1_1", align_bytes=64)
+        nc.sync.dma_start(wg1_rows[:], wg1)
+        load_page(2)
+        w1_raw = {(a, 0): load_rows("w1_raw%d0" % a, w1, a, 0, KP) for a in range(2)}
+        idx1 = load_list("idx1", offs)
+        t_words = []
+        for a in range(2):
+            words = raw_tile("t_words%d" % a, [P, T], U32)
+            nc.sync.dma_start(words[:].bitcast(I32), tab_words[a].rearrange("p n i -> p (n i)").bitcast(I32))
+            t_words.append(words)
+        for q in range(4):
+            nc.sync.dma_start(t_scales[32 * q : 32 * q + 8, :].bitcast(I32), tab_scales[:, 4 * q : 4 * q + 4, :].bitcast(I32))
+        load_page(3)
+        idx3 = load_list("idx3", offs3)
+        idx5 = load_list("idx5", offs5)
+        gains = kept("gains", [P, 2, PACK], F32)
+        nc.sync.dma_start(gains[:], gain.rearrange("(b p t) -> p b t", p=P, t=PACK))
+
+        def grouped_tile(name):
+            return ring.tile([P, 4 * KP], BF16, name=name, tag="grouped", bufs=3, align_bytes=64)
+
+        def round_dealt(copy, grouped, raw, m0):
+            copy(
+                out=grouped[:].rearrange("p (t m j) -> p m j t", t=PACK, j=PACK)[:, m0 : m0 + raw.shape[2] // PACK, :, :],
+                in_=raw[:].rearrange("p j (m t) -> p m j t", t=PACK),
+            )
+
+        def quantize(name, src, codes):
+            scales = kept(name + "_scales", [P, codes.shape[1]], U8)
+            nc.vector.quantize_mx(out=codes.bitcast(FP8X4), scales=scales[:], in_=src)
+            return codes, scales
+
+        def codes_tile(name, width, tag=None):
+            return keep.tile([P, width], U32, name=name, tag=tag or name, align_bytes=64)
+
+        def gather(name, window, idx, dtype):
+            tile = kept(name, [P, S], dtype)
+            nc.vector.tensor_copy(tile[:], window[:].indirect(idx[:]))
+            return tile
+
+        def deal_w2(b, words_tag, scales_tag):
+            words = keep.tile([P, 2 * KP], U8, name="w2_dealt%d" % b, tag=words_tag, align_bytes=64)
+            scales = keep.tile([P, KP], U8, name="w2_sc%d" % b, tag=scales_tag, align_bytes=64)
+            nc.vector.tensor_copy(
+                out=words[:].rearrange("p (t m e) -> p m t e", t=PACK, e=2),
+                in_=w2_raw[:, 2 * KP * b : 2 * KP * (b + 1)].rearrange("p (m t e) -> p m t e", t=PACK, e=2),
+            )
+            nc.vector.tensor_copy(
+                out=scales[:].rearrange("p (t m) -> p m t", t=PACK),
+                in_=w2_sc_raw[:, KP * b : KP * (b + 1)].rearrange("p (m t) -> p m t", t=PACK),
+            )
+            return words, scales
+
+        def work_tile(name, tag):
+            return keep.tile([P, S], F32, name=name, tag=tag, align_bytes=64)
+
+        late_values = {}
+
+        def values_tile(i, stream):
+            if i < PACK:
+                return work_tile("h%d_%d" % (stream, i), "h%d_%d" % (stream, i))[:]
+            if i not in late_values:
+                late_values[i] = keep.tile([P, 2, S], F32, name="values%d" % i, tag=PAGE_SLOT[i - 1], align_bytes=64)
+            return late_values[i][:, stream - 1, :]
+
+        def side_size(i, w3q):
+            t = i % PACK
+            cols = slice(P * t, P * (t + 1))
+            side = bank("side%d" % i, i % 2, [P, S])
+            nc.tensor.matmul_mx(out=side[:], lhsT=w3q[0][:, cols].bitcast(FP8X4), lhsT_scale=w3q[1][:, cols],
+                                rhs=v2_words[:].bitcast(FP8X4), rhs_scale=v2_scales[:], start=True, stop=True)
+            size = work_tile("size%d" % i, "size%d" % t)
+            nc.scalar.activation(size[:], side[:], ACT.Abs)
+            return size
+
+        def stream2_values(i, w2q, size):
+            t = i % PACK
+            cols = slice(P * t, P * (t + 1))
+            base = bank("base%d" % i, 2 + i % 2, [P, S])
+            nc.tensor.matmul_mx(out=base[:], lhsT=w2q[0][:, 2 * P * t : 2 * P * (t + 1)].bitcast(FP4X4), lhsT_scale=w2q[1][:, cols],
+                                rhs=v2_words[:].bitcast(FP8X4), rhs_scale=v2_scales[:], start=True, stop=True)
+            h2 = values_tile(i, 2)
+            nc.vector.tensor_tensor(h2, base[:], size[:], ALU.subtract)
+            return h2
+
+        def stream1_values(i, w1q):
+            t = i % PACK
+            cols = slice(P * t, P * (t + 1))
+            pre = bank("pre%d" % i, 4 + t, [P, S])
+            for a in range(2):
+                nc.tensor.matmul_mx(out=pre[:], lhsT=w1q[a][0][:, cols].bitcast(FP8X4), lhsT_scale=w1q[a][1][:, cols],
+                                    rhs=v_words[a][:].bitcast(FP8X4), rhs_scale=v_scales[4 * a : P, :],
+                                    start=(a == 0), stop=(a == 1))
+            h1 = values_tile(i, 1)
+            nc.scalar.activation(h1, pre[:], ACT.Gelu_apprx_tanh)
+            return h1
+
+        def put(i, idx, values, gate):
+            nc.vector.tensor_tensor(pages[i][:].indirect(idx[:]), values, gate[i % PACK], ALU.mult)
+
+        def picked_tile(i, slot):
+            return keep.tile([P, NP], F32, name="picked%d" % i, tag="picked%d" % slot)
+
+        def fetch(i, picked, c0, width):
+            cols = slice(c0, c0 + width)
+            nc.vector.tensor_copy(picked[:, cols], pages[i][:].indirect(idx5[:, c0 // 16 : (c0 + width) // 16]))
+
+        def squash(picked, c0, width):
+            nc.scalar.activation(picked[:, c0 : c0 + width], picked[:, c0 : c0 + width], ACT.Tanh)
+
+        def round_w1(b):
+            result = []
+            for a in range(2):
+                grouped = grouped_tile("w1_grouped%d%d" % (a, b))
+                round_dealt(nc.scalar.copy, grouped, w1_raw[(a, b)], 0)
+                result.append(grouped[:])
+            return result
+
+        def quantize_all(name, grouped, tag):
+            codes = codes_tile(name, len(grouped) * KP, tag)
+            return [quantize("%s%d" % (name, a), src, codes[:, KP * a : KP * (a + 1)]) for a, src in enumerate(grouped)]
+
+        v2_words = gather("v2_words", t2_words, idx2, U32)
+        v2_scales = gather("v2_scales", t2_scales, idx2, U8)
+        grouped = grouped_tile("w3_grouped0")
+        round_dealt(nc.scalar.copy, grouped, w3_head[0], 0)
+        round_dealt(nc.vector.tensor_copy, grouped, w3_head[1], P // 2)
+        w3q = quantize("w3q0", grouped[:], codes_tile("w3q0", KP)[:])
+        w2q = deal_w2(0, "w2_dealt0", "w2_sc0")
+        turned = turn_gate("gate2", wg2_rows)
+        h2 = {}
+        gate2 = []
+        for i in range(PACK):
+            h2[i] = stream2_values(i, w2q, side_size(i, w3q))
+            gate2.append(deal_gate("gate2", turned, i))
+            if i < PACK - 1:
+                put(i, idx4, h2[i], gate2)
+        w1q = quantize_all("w1q_lo", round_w1(0), None)
+        turned = turn_gate("gate1", wg1_rows)
+        gate1 = [deal_gate("gate1", turned, t) for t in range(PACK)]
+        v_words = [gather("v_words%d" % a, t_words[a], idx1, U32) for a in range(2)]
+        v_scales = gather("v_scales", t_scales, idx1, U8)
+        h1 = {i: stream1_values(i, w1q) for i in range(PACK)}
+        put(PACK - 1, idx4, h2[PACK - 1], gate2)
+
+        w3_tail = load_rows("w3_tail", w3, 0, KP, KP)
+        for a in range(2):
+            w1_raw[(a, 1)] = load_rows("w1_raw%d1" % a, w1, a, KP, KP)
+        for i in range(PACK, 2 * PACK - 1):
+            load_page(i)
+        w4_w = kept("w4_w", [P, 2, 2 * N], U8)
+        nc.sync.dma_start(w4_w[:].bitcast(I32), w4_words.rearrange("a p n -> p a n").bitcast(I32))
+        for q in range(4):
+            nc.sync.dma_start(w4_sc[32 * q : 32 * q + 4, :, :].bitcast(I32),
+                              w4_scales[:, 4 * q : 4 * q + 4, :].rearrange("a q n -> q a n").bitcast(I32))
+        w5_raw = [load_rows("w5_raw%d" % b, w5, b, 0, N) for b in range(2)]
+        load_page(7)
+
+        w3_grouped = grouped_tile("w3_grouped1")
+        round_dealt(nc.scalar.copy, w3_grouped, w3_tail, 0)
+        w1_grouped = round_w1(1)
+
+        x_rows = kept("x_rows", [P, PACK, NP], BF16)
+        for i in range(PACK):
+            put(i, idx3, h1[i], gate1)
+            picked = picked_tile(i, i % 3)
+            fetch(i, picked, 0, NP)
+            if i == 1:
+                w2q = deal_w2(1, PAGE_SLOT[1], PAGE_SLOT[0])
+            if i == 2:
+                w3q, *w1q = quantize_all("wq_hi", [w3_grouped[:]] + w1_grouped, PAGE_SLOT[2])
+                sizes = {PACK: side_size(PACK, w3q)}
+            if i == PACK - 1:
+                h1[PACK] = stream1_values(PACK, w1q)
+                h2[PACK] = stream2_values(PACK, w2q, sizes[PACK])
+                for k in range(PACK + 1, 2 * PACK):
+                    sizes[k] = side_size(k, w3q)
+            for c0 in (0, KP):
+                squash(picked, c0, KP)
+            for c0 in (0, KP):
+                nc.scalar.activation(x_rows[:, i, c0 : c0 + KP], picked[:, c0 : c0 + KP], ACT.Copy, scale=gains[:, 0, i : i + 1])
+
+        x_lo = kept("x_lo", [P, NP, PACK], BF16)
+        for c in range(NCH):
+            nc.scalar.copy(
+                out=x_lo[:, CH * c : CH * (c + 1), :].rearrange("p (c i) t -> p c t i", i=8),
+                in_=x_rows[:, :, CH * c : CH * (c + 1)].rearrange("p t (c i) -> p c t i", i=8),
+            )
+        w5_both = keep.tile([P, 2, PACK * N], BF16, name="w5_grouped", tag="x_rows", align_bytes=64)
+        w5_grouped = [w5_both[:, b, :] for b in range(2)]
+
+        x_hi = [kept("x_hi%d" % c, [P, CH, PACK], BF16) for c in range(NCH)]
+        last = 2 * PACK - 1
+        for i in range(PACK, last):
+            t = i % PACK
+            put(i, idx4, h2[i], gate2)
+            put(i, idx3, h1[i], gate1)
+            picked = picked_tile(i, i % 3)
+            fetch(i, picked, 0, NP)
+            h1[i + 1] = stream1_values(i + 1, w1q)
+            h2[i + 1] = stream2_values(i + 1, w2q, sizes[i + 1])
+            for c0 in (0, KP):
+                squash(picked, c0, KP)
+            for c in range(NCH):
+                nc.scalar.activation(x_hi[c][:, :, t], picked[:, CH * c : CH * (c + 1)], ACT.Copy, scale=gains[:, 1, t : t + 1])
+            if t < 2:
+                nc.scalar.copy(
+                    out=w5_grouped[t].rearrange("p (c i j) -> p c j i", i=4, j=PACK),
+                    in_=w5_raw[t][:].rearrange("p j (c i) -> p c j i", i=4),
+                )
+        xq_lo = quantize("xq_lo", x_lo[:].rearrange("p c t -> p (c t)"), codes_tile("xq_lo", NP, PAGE_SLOT[4])[:])
+        w5q = quantize_all("w5q", w5_grouped, PAGE_SLOT[5])
+        put(last, idx4, h2[last], gate2)
+        put(last, idx3, h1[last], gate1)
+
+        def passes(acc, second, pair, b, xq, c0):
+            for u in range(2):
+                n = 2 * pair + u
+                cols = slice(P * n, P * (n + 1))
+                if second:
+                    lhsT, lhsT_scale = w5q[b][0][:, cols].bitcast(FP8X4), w5q[b][1][:, cols]
+                else:
+                    lhsT, lhsT_scale = w4_w[:, b, 2 * P * n : 2 * P * (n + 1)].bitcast(FP4X4), w4_sc[:, b, cols]
+                nc.tensor.matmul_mx(out=acc[:, u, :], lhsT=lhsT, lhsT_scale=lhsT_scale,
+                                    rhs=xq[0][:, c0 : c0 + CH].bitcast(FP8X4), rhs_scale=xq[1][:, c0 : c0 + CH],
+                                    start=(b == 0 and u == 0), stop=(b == 1 and u == 1))
+
+        accs = {}
+
+        def open_chunk(c):
+            for pair in range(2):
+                for second in (1, 0):
+                    acc = bank("acc%d%d%d" % (c, pair, second), 4 * (c % 2) + 2 * pair + second, [P, 2, CH])
+                    accs[(c, pair, second)] = acc
+                    passes(acc, second, pair, 0, xq_lo, CH * c)
+
+        diffs = {}
+
+        def close_chunk(c, xq):
+            for pair in range(2):
+                for second in (1, 0):
+                    passes(accs[(c, pair, second)], second, pair, 1, xq, 0)
+                slot = 2 * (c % 2) + pair
+                size = work_tile("y2abs%d%d" % (c, pair), "size%d" % slot)
+                nc.scalar.activation(size[:], accs[(c, pair, 1)][:].rearrange("p u c -> p (u c)"), ACT.Abs)
+                diff = work_tile("diff%d%d" % (c, pair), "h2_%d" % slot)
+                nc.vector.tensor_tensor(diff[:], accs[(c, pair, 0)][:].rearrange("p u c -> p (u c)"), size[:], ALU.subtract)
+                diffs[(c, pair)] = diff
+
+        def store_chunk(c):
+            for pair in range(2):
+                diff = diffs[(c, pair)]
+                result = raw_tile("result%d%d" % (c, pair), [P, S], F32)
+                if 2 * c + pair >= 2 * NCH - ABS_ON_VECTOR:
+                    nc.vector.scalar_tensor_tensor(result[:], diff[:], -1.0, diff[:], ALU.mult, ALU.max)
+                else:
+                    nc.scalar.activation(result[:], diff[:], ACT.Abs)
+                nc.sync.dma_start(
+                    out[2 * P * pair : 2 * P * (pair + 1), CH * c : CH * (c + 1)].rearrange("(u p) c -> p u c", p=P),
+                    result[:].rearrange("p (u c) -> p u c", u=2),
+                )
+
+        open_chunk(0)
+        open_chunk(1)
+        xq_hi = []
+        picked = picked_tile(last, (last - 1) % 3)
+        for c in range(NCH):
+            cols = slice(CH * (c % 2), CH * (c % 2 + 1))
+            nc.vector.tensor_copy(picked[:, cols], pages[last][:].indirect(idx5[:, CH * c // 16 : CH * (c + 1) // 16]))
+            nc.scalar.activation(picked[:, cols], picked[:, cols], ACT.Tanh)
+            if c in ROUND_ON_VECTOR:
+                nc.vector.tensor_scalar(x_hi[c][:, :, PACK - 1], picked[:, cols], gains[:, 1, PACK - 1 : PACK], None, ALU.mult)
+            else:
+                nc.scalar.activation(x_hi[c][:, :, PACK - 1], picked[:, cols], ACT.Copy, scale=gains[:, 1, PACK - 1 : PACK])
+            xq_hi.append(quantize("xq_hi%d" % c, x_hi[c][:].rearrange("p c t -> p (c t)"), codes_tile("xq_hi%d" % c, CH)[:]))
+        for c in range(NCH):
+            close_chunk(c, xq_hi[c])
+            if c + 2 < NCH:
+                open_chunk(c + 2)
+            if c > 0:
+                store_chunk(c - 1)
+        store_chunk(NCH - 1)

@@ -22,9 +22,13 @@ PACK = 4
 KP = P * PACK
 CH = 256
 NCH = NP // CH
-ROUND_ON_VECTOR = (0, 1, 2, 3)
-ABS_ON_VECTOR = 3
-PAGE_SLOT = ["slot%d" % i for i in range(8)]
+HEAD_SPLIT = 40
+ROUND_ON_VECTOR = (0, 2, 3)
+ABS_ON_VECTOR = 2
+PAGE_SLOT = ["page0", "page1", "page2", "page3", "w3_head", "w1_raw00", "t_words0", "w1_raw10"]
+H2_SLOT = [PAGE_SLOT[i] for i in (2, 3, 4, 6)]
+W5_SLOT = ["t_words1", "w3_tail"]
+RESULT_SLOT = ["w1_raw01", "w1_raw11", "t_words1", "w3_tail", "w1_raw00", "w3_head", "page1", "page2"]
 
 
 def tile_list_crock_slot_scores_kernel(
@@ -46,8 +50,12 @@ def tile_list_crock_slot_scores_kernel(
             nc.sync.dma_start(tile[:], src)
             return tile
 
-        def raw_tile(name, shape, dtype):
-            return ring.tile(shape, dtype, name=name, tag="raw", bufs=5, align_bytes=64)
+        def raw_tile(name, shape, dtype, tag=None):
+            return keep.tile(shape, dtype, name=name, tag=tag or name, align_bytes=64)
+
+        def load_scale_rows(plane, scales, q):
+            rows = scales[0, 4 * q : 4 * q + 4, :].bitcast(I32)
+            nc.sync.dma_start(plane[32 * q : 32 * (q + 1), :].bitcast(I32), rows.unsqueeze(0).broadcast_to([8, 4, rows.shape[1]]))
 
         def bank(name, index, shape):
             return psum.tile(shape, F32, name=name, tag="bank%d" % index)
@@ -56,8 +64,6 @@ def tile_list_crock_slot_scores_kernel(
         w2_sc_raw = kept("w2_sc_raw", [P, H], U8)
         t_scales = kept("t_scales", [P, T], U8)
         w4_sc = kept("w4_sc", [P, 2, N], U8)
-        nc.vector.memset(t2_scales[:].bitcast(I32), 0)
-        nc.vector.memset(w2_sc_raw[:].bitcast(I32), 0)
         nc.vector.memset(t_scales[:].bitcast(I32), 0)
         nc.vector.memset(w4_sc[:].bitcast(I32), 0)
 
@@ -65,8 +71,8 @@ def tile_list_crock_slot_scores_kernel(
         nc.sync.dma_start(t2_words[:].bitcast(I32), tab2_words[0].rearrange("p n i -> p (n i)").bitcast(I32))
         idx2 = load_list("idx2", offs2)
 
-        def load_rows(name, w, a, c0, width):
-            raw = raw_tile(name, [P, PACK, width], F32)
+        def load_rows(name, w, a, c0, width, tag=None):
+            raw = raw_tile(name, [P, PACK, width], F32, tag)
             nc.sync.dma_start(raw[:], w[KP * a : KP * (a + 1), c0 : c0 + width].rearrange("(p j) c -> p j c", j=PACK))
             return raw
 
@@ -79,11 +85,12 @@ def tile_list_crock_slot_scores_kernel(
                 nc.tensor.transpose(turned[:, jt, :], rows[:, P * jt : P * (jt + 1)], identity[:])
             return turned
 
-        def deal_gate(name, turned, t):
-            spread = keep.tile([P, PACK, 4, 32], F32, name="%s_spread%d" % (name, t), tag="spread%d" % (t % 2))
-            nc.scalar.copy(
-                out=spread[:],
-                in_=turned[:].rearrange("p jt (q t) -> p jt q t", t=PACK)[:, :, :, t].unsqueeze(2).broadcast_to([P, PACK, 4, 32]),
+        def deal_gate(name, turned, t, tag):
+            spread = keep.tile([P, PACK, 4, 32], F32, name="%s_spread%d" % (name, t), tag=tag, align_bytes=64)
+            nc.scalar.activation(
+                spread[:],
+                turned[:].rearrange("p jt (q t) -> p jt q t", t=PACK)[:, :, :, t].unsqueeze(2).broadcast_to([P, PACK, 4, 32]),
+                ACT.Copy,
             )
             back = bank("%s_back%d" % (name, t), 5 + t % 2, [P, S])
             for jt in range(PACK):
@@ -99,23 +106,22 @@ def tile_list_crock_slot_scores_kernel(
             pages[i] = keep.tile([P, T2], F32, name="page%d" % i, tag=PAGE_SLOT[i], align_bytes=64)
             nc.sync.dma_start(pages[i][:], page0[KP * b : KP * (b + 1), :].rearrange("(p t) c -> t p c", t=PACK)[t])
 
-        w3_head = [load_rows("w3_head0", w3, 0, 0, KP // 2)]
         for q in range(4):
-            nc.sync.dma_start(t2_scales[32 * q : 32 * q + 4, :].bitcast(I32), tab2_scales[0, 4 * q : 4 * q + 4, :].bitcast(I32))
-        w3_head.append(load_rows("w3_head1", w3, 0, KP // 2, KP // 2))
+            load_scale_rows(t2_scales, tab2_scales, q)
         wg2_rows = keep.tile([P, S], F32, name="wg2_rows", tag="h1_0", align_bytes=64)
         nc.sync.dma_start(wg2_rows[:], wg2)
-        w2_raw = kept("w2_raw", [P, 2 * H], U8)
-        nc.sync.dma_start(w2_raw[:].bitcast(I32), w2_words[0].bitcast(I32))
+        w3_head = load_rows("w3_head", w3, 0, 0, KP)
+        w2_lo = kept("w2_lo", [P, 2 * KP], U8)
+        nc.sync.dma_start(w2_lo[:].bitcast(I32), w2_words[0, :, 0 : 2 * KP].bitcast(I32))
         for q in range(4):
-            nc.sync.dma_start(w2_sc_raw[32 * q : 32 * q + 4, :].bitcast(I32), w2_scales[0, 4 * q : 4 * q + 4, :].bitcast(I32))
-        idx4 = load_list("idx4", offs4)
+            load_scale_rows(w2_sc_raw, w2_scales, q)
         load_page(0)
+        idx4 = load_list("idx4", offs4)
         load_page(1)
-        wg1_rows = keep.tile([P, S], F32, name="wg1_rows", tag="h1_1", align_bytes=64)
-        nc.sync.dma_start(wg1_rows[:], wg1)
         load_page(2)
         w1_raw = {(a, 0): load_rows("w1_raw%d0" % a, w1, a, 0, KP) for a in range(2)}
+        wg1_rows = keep.tile([P, S], F32, name="wg1_rows", tag="h1_1", align_bytes=64)
+        nc.sync.dma_start(wg1_rows[:], wg1)
         idx1 = load_list("idx1", offs)
         t_words = []
         for a in range(2):
@@ -125,18 +131,13 @@ def tile_list_crock_slot_scores_kernel(
         for q in range(4):
             nc.sync.dma_start(t_scales[32 * q : 32 * q + 8, :].bitcast(I32), tab_scales[:, 4 * q : 4 * q + 4, :].bitcast(I32))
         load_page(3)
-        idx3 = load_list("idx3", offs3)
-        idx5 = load_list("idx5", offs5)
-        gains = kept("gains", [P, 2, PACK], F32)
-        nc.sync.dma_start(gains[:], gain.rearrange("(b p t) -> p b t", p=P, t=PACK))
-
         def grouped_tile(name):
             return ring.tile([P, 4 * KP], BF16, name=name, tag="grouped", bufs=3, align_bytes=64)
 
-        def round_dealt(copy, grouped, raw, m0):
+        def round_dealt(copy, grouped, raw, m0=0, m1=P):
             copy(
-                out=grouped[:].rearrange("p (t m j) -> p m j t", t=PACK, j=PACK)[:, m0 : m0 + raw.shape[2] // PACK, :, :],
-                in_=raw[:].rearrange("p j (m t) -> p m j t", t=PACK),
+                out=grouped[:].rearrange("p (t m j) -> p m j t", t=PACK, j=PACK)[:, m0:m1, :, :],
+                in_=raw[:].rearrange("p j (m t) -> p m j t", t=PACK)[:, m0:m1, :, :],
             )
 
         def quantize(name, src, codes):
@@ -152,49 +153,69 @@ def tile_list_crock_slot_scores_kernel(
             nc.vector.tensor_copy(tile[:], window[:].indirect(idx[:]))
             return tile
 
-        def deal_w2(b, words_tag, scales_tag):
-            words = keep.tile([P, 2 * KP], U8, name="w2_dealt%d" % b, tag=words_tag, align_bytes=64)
-            scales = keep.tile([P, KP], U8, name="w2_sc%d" % b, tag=scales_tag, align_bytes=64)
+        def first_operands(name, grouped, t0, t1):
+            count = t1 - t0
+            w3q = quantize("w3q_" + name, grouped[:, KP * t0 : KP * t1], codes_tile("w3q_" + name, P * count)[:])
+            words = kept("w2_dealt_" + name, [P, 2 * P * count], U8)
+            scales = kept("w2_sc_" + name, [P, P * count], U8)
             nc.vector.tensor_copy(
-                out=words[:].rearrange("p (t m e) -> p m t e", t=PACK, e=2),
-                in_=w2_raw[:, 2 * KP * b : 2 * KP * (b + 1)].rearrange("p (m t e) -> p m t e", t=PACK, e=2),
+                out=words[:].rearrange("p (t m e) -> p m t e", t=count, e=2),
+                in_=w2_lo[:].rearrange("p (m t e) -> p m t e", t=PACK, e=2)[:, :, t0:t1, :],
             )
             nc.vector.tensor_copy(
-                out=scales[:].rearrange("p (t m) -> p m t", t=PACK),
-                in_=w2_sc_raw[:, KP * b : KP * (b + 1)].rearrange("p (m t) -> p m t", t=PACK),
+                out=scales[:].rearrange("p (t m) -> p m t", t=count),
+                in_=w2_sc_raw[:, 0:KP].rearrange("p (m t) -> p m t", t=PACK)[:, :, t0:t1],
             )
-            return words, scales
+            return [
+                (w3q[0][:, P * u : P * (u + 1)], w3q[1][:, P * u : P * (u + 1)],
+                 words[:, 2 * P * u : 2 * P * (u + 1)], scales[:, P * u : P * (u + 1)])
+                for u in range(count)
+            ]
 
         def work_tile(name, tag):
             return keep.tile([P, S], F32, name=name, tag=tag, align_bytes=64)
 
-        late_values = {}
-
-        def values_tile(i, stream):
-            if i < PACK:
-                return work_tile("h%d_%d" % (stream, i), "h%d_%d" % (stream, i))[:]
-            if i not in late_values:
-                late_values[i] = keep.tile([P, 2, S], F32, name="values%d" % i, tag=PAGE_SLOT[i - 1], align_bytes=64)
-            return late_values[i][:, stream - 1, :]
-
-        def side_size(i, w3q):
-            t = i % PACK
-            cols = slice(P * t, P * (t + 1))
+        def stream2_values(i, operands):
+            w3_codes, w3_scales, w2_codes, w2_plane = operands
             side = bank("side%d" % i, i % 2, [P, S])
-            nc.tensor.matmul_mx(out=side[:], lhsT=w3q[0][:, cols].bitcast(FP8X4), lhsT_scale=w3q[1][:, cols],
+            nc.tensor.matmul_mx(out=side[:], lhsT=w3_codes.bitcast(FP8X4), lhsT_scale=w3_scales,
                                 rhs=v2_words[:].bitcast(FP8X4), rhs_scale=v2_scales[:], start=True, stop=True)
-            size = work_tile("size%d" % i, "size%d" % t)
+            size = work_tile("size%d" % i, "size%d" % i)
             nc.scalar.activation(size[:], side[:], ACT.Abs)
-            return size
+            base = bank("base%d" % i, (i + 2) % 4, [P, S])
+            nc.tensor.matmul_mx(out=base[:], lhsT=w2_codes.bitcast(FP4X4), lhsT_scale=w2_plane,
+                                rhs=v2_words[:].bitcast(FP8X4), rhs_scale=v2_scales[:], start=True, stop=True)
+            h2 = work_tile("h2_%d" % i, "h2_%d" % (i % 2))[:]
+            nc.vector.tensor_tensor(h2, base[:], size[:], ALU.subtract)
+            return h2
 
-        def stream2_values(i, w2q, size):
+        def stream2_turned(w3q):
+            minus, sizes = [], []
+            for jt in range(PACK):
+                entries = slice(P * jt, P * (jt + 1))
+                base = bank("base_turned%d" % jt, jt, [P, KP])
+                nc.tensor.matmul_mx(out=base[:], lhsT=v2_words[:, entries].bitcast(FP8X4), lhsT_scale=v2_scales[:, entries],
+                                    rhs=w2_hi[:].bitcast(FP4X4), rhs_scale=w2_sc_raw[:, KP : 2 * KP], start=True, stop=True)
+                minus.append(work_tile("minus_base%d" % jt, "minus%d" % jt))
+                nc.scalar.activation(minus[jt][:].rearrange("p (t m) -> p t m", t=PACK), base[:].rearrange("p (m t) -> p t m", t=PACK), ACT.Copy, scale=-1.0)
+            for jt in range(PACK):
+                entries = slice(P * jt, P * (jt + 1))
+                side = bank("side_turned%d" % jt, jt, [P, KP])
+                nc.tensor.matmul_mx(out=side[:], lhsT=v2_words[:, entries].bitcast(FP8X4), lhsT_scale=v2_scales[:, entries],
+                                    rhs=w3q[0].bitcast(FP8X4), rhs_scale=w3q[1][:], start=True, stop=True)
+                sizes.append(work_tile("size_turned%d" % jt, "size%d" % jt))
+                nc.scalar.activation(sizes[jt][:], side[:], ACT.Abs)
+            return list(zip(sizes, minus))
+
+        def stream2_turn_back(i, parts):
             t = i % PACK
             cols = slice(P * t, P * (t + 1))
-            base = bank("base%d" % i, 2 + i % 2, [P, S])
-            nc.tensor.matmul_mx(out=base[:], lhsT=w2q[0][:, 2 * P * t : 2 * P * (t + 1)].bitcast(FP4X4), lhsT_scale=w2q[1][:, cols],
-                                rhs=v2_words[:].bitcast(FP8X4), rhs_scale=v2_scales[:], start=True, stop=True)
-            h2 = values_tile(i, 2)
-            nc.vector.tensor_tensor(h2, base[:], size[:], ALU.subtract)
+            total = bank("total%d" % i, i % 2, [P, S])
+            for jt in range(PACK):
+                for k in range(2):
+                    nc.tensor.matmul(total[:, P * jt : P * (jt + 1)], parts[jt][k][:, cols], identity[:], start=(k == 0), stop=(k == 1), is_transpose=True)
+            h2 = work_tile("h2_%d" % i, H2_SLOT[t])[:]
+            nc.scalar.activation(h2, total[:], ACT.Copy, scale=-1.0)
             return h2
 
         def stream1_values(i, w1q):
@@ -205,7 +226,7 @@ def tile_list_crock_slot_scores_kernel(
                 nc.tensor.matmul_mx(out=pre[:], lhsT=w1q[a][0][:, cols].bitcast(FP8X4), lhsT_scale=w1q[a][1][:, cols],
                                     rhs=v_words[a][:].bitcast(FP8X4), rhs_scale=v_scales[4 * a : P, :],
                                     start=(a == 0), stop=(a == 1))
-            h1 = values_tile(i, 1)
+            h1 = work_tile("h1_%d" % i, "h1_%d" % t)[:]
             nc.scalar.activation(h1, pre[:], ACT.Gelu_apprx_tanh)
             return h1
 
@@ -226,7 +247,7 @@ def tile_list_crock_slot_scores_kernel(
             result = []
             for a in range(2):
                 grouped = grouped_tile("w1_grouped%d%d" % (a, b))
-                round_dealt(nc.scalar.copy, grouped, w1_raw[(a, b)], 0)
+                round_dealt(nc.scalar.copy, grouped, w1_raw[(a, b)])
                 result.append(grouped[:])
             return result
 
@@ -237,29 +258,34 @@ def tile_list_crock_slot_scores_kernel(
         v2_words = gather("v2_words", t2_words, idx2, U32)
         v2_scales = gather("v2_scales", t2_scales, idx2, U8)
         grouped = grouped_tile("w3_grouped0")
-        round_dealt(nc.scalar.copy, grouped, w3_head[0], 0)
-        round_dealt(nc.vector.tensor_copy, grouped, w3_head[1], P // 2)
-        w3q = quantize("w3q0", grouped[:], codes_tile("w3q0", KP)[:])
-        w2q = deal_w2(0, "w2_dealt0", "w2_sc0")
+        round_dealt(nc.scalar.copy, grouped, w3_head, 0, HEAD_SPLIT)
+        round_dealt(nc.vector.tensor_copy, grouped, w3_head, HEAD_SPLIT, P)
+        operands = first_operands("first", grouped, 0, 1) + first_operands("rest", grouped, 1, PACK)
         turned = turn_gate("gate2", wg2_rows)
         h2 = {}
         gate2 = []
         for i in range(PACK):
-            h2[i] = stream2_values(i, w2q, side_size(i, w3q))
-            gate2.append(deal_gate("gate2", turned, i))
+            h2[i] = stream2_values(i, operands[i])
+            gate2.append(deal_gate("gate2", turned, i, "spread0" if i == 0 else "w2_lo"))
             if i < PACK - 1:
                 put(i, idx4, h2[i], gate2)
         w1q = quantize_all("w1q_lo", round_w1(0), None)
         turned = turn_gate("gate1", wg1_rows)
-        gate1 = [deal_gate("gate1", turned, t) for t in range(PACK)]
+        gate1 = [deal_gate("gate1", turned, t, "spread%d" % (t % 2)) for t in range(PACK)]
         v_words = [gather("v_words%d" % a, t_words[a], idx1, U32) for a in range(2)]
         v_scales = gather("v_scales", t_scales, idx1, U8)
         h1 = {i: stream1_values(i, w1q) for i in range(PACK)}
         put(PACK - 1, idx4, h2[PACK - 1], gate2)
 
         w3_tail = load_rows("w3_tail", w3, 0, KP, KP)
-        for a in range(2):
-            w1_raw[(a, 1)] = load_rows("w1_raw%d1" % a, w1, a, KP, KP)
+        w2_hi = kept("w2_hi", [P, 2 * KP], U8)
+        nc.sync.dma_start(w2_hi[:].bitcast(I32), w2_words[0, :, 2 * KP : 4 * KP].bitcast(I32))
+        w1_raw[(0, 1)] = load_rows("w1_raw01", w1, 0, KP, KP)
+        idx3 = load_list("idx3", offs3)
+        w1_raw[(1, 1)] = load_rows("w1_raw11", w1, 1, KP, KP)
+        idx5 = load_list("idx5", offs5)
+        gains = kept("gains", [P, 2, PACK], F32)
+        nc.sync.dma_start(gains[:], gain.rearrange("(b p t) -> p b t", p=P, t=PACK))
         for i in range(PACK, 2 * PACK - 1):
             load_page(i)
         w4_w = kept("w4_w", [P, 2, 2 * N], U8)
@@ -267,34 +293,34 @@ def tile_list_crock_slot_scores_kernel(
         for q in range(4):
             nc.sync.dma_start(w4_sc[32 * q : 32 * q + 4, :, :].bitcast(I32),
                               w4_scales[:, 4 * q : 4 * q + 4, :].rearrange("a q n -> q a n").bitcast(I32))
-        w5_raw = [load_rows("w5_raw%d" % b, w5, b, 0, N) for b in range(2)]
+        w5_raw = [load_rows("w5_raw%d" % b, w5, b, 0, N, W5_SLOT[b]) for b in range(2)]
         load_page(7)
 
         w3_grouped = grouped_tile("w3_grouped1")
-        round_dealt(nc.scalar.copy, w3_grouped, w3_tail, 0)
-        w1_grouped = round_w1(1)
+        round_dealt(nc.scalar.copy, w3_grouped, w3_tail)
+
+        for i in range(PACK):
+            put(i, idx3, h1[i], gate1)
+            if i == 0:
+                parts = stream2_turned(quantize("w3q1", w3_grouped[:], codes_tile("w3q1", KP, "h1_0")[:]))
+        w1q = quantize_all("w1q_hi", round_w1(1), None)
+
+        def late_values(i):
+            h2[i] = stream2_turn_back(i, parts)
+            h1[i] = stream1_values(i, w1q)
 
         x_rows = kept("x_rows", [P, PACK, NP], BF16)
         for i in range(PACK):
-            put(i, idx3, h1[i], gate1)
             picked = picked_tile(i, i % 3)
             fetch(i, picked, 0, NP)
-            if i == 1:
-                w2q = deal_w2(1, PAGE_SLOT[1], PAGE_SLOT[0])
-            if i == 2:
-                w3q, *w1q = quantize_all("wq_hi", [w3_grouped[:]] + w1_grouped, PAGE_SLOT[2])
-                sizes = {PACK: side_size(PACK, w3q)}
-            if i == PACK - 1:
-                h1[PACK] = stream1_values(PACK, w1q)
-                h2[PACK] = stream2_values(PACK, w2q, sizes[PACK])
-                for k in range(PACK + 1, 2 * PACK):
-                    sizes[k] = side_size(k, w3q)
+            if i >= 2:
+                late_values(i + 2)
             for c0 in (0, KP):
                 squash(picked, c0, KP)
             for c0 in (0, KP):
                 nc.scalar.activation(x_rows[:, i, c0 : c0 + KP], picked[:, c0 : c0 + KP], ACT.Copy, scale=gains[:, 0, i : i + 1])
 
-        x_lo = kept("x_lo", [P, NP, PACK], BF16)
+        x_lo = keep.tile([P, NP, PACK], BF16, name="x_lo", tag=PAGE_SLOT[0], align_bytes=64)
         for c in range(NCH):
             nc.scalar.copy(
                 out=x_lo[:, CH * c : CH * (c + 1), :].rearrange("p (c i) t -> p c t i", i=8),
@@ -311,8 +337,8 @@ def tile_list_crock_slot_scores_kernel(
             put(i, idx3, h1[i], gate1)
             picked = picked_tile(i, i % 3)
             fetch(i, picked, 0, NP)
-            h1[i + 1] = stream1_values(i + 1, w1q)
-            h2[i + 1] = stream2_values(i + 1, w2q, sizes[i + 1])
+            if i > PACK:
+                late_values(i + 1)
             for c0 in (0, KP):
                 squash(picked, c0, KP)
             for c in range(NCH):
@@ -322,9 +348,9 @@ def tile_list_crock_slot_scores_kernel(
                     out=w5_grouped[t].rearrange("p (c i j) -> p c j i", i=4, j=PACK),
                     in_=w5_raw[t][:].rearrange("p j (c i) -> p c j i", i=4),
                 )
-        xq_lo = quantize("xq_lo", x_lo[:].rearrange("p c t -> p (c t)"), codes_tile("xq_lo", NP, PAGE_SLOT[4])[:])
-        w5q = quantize_all("w5q", w5_grouped, PAGE_SLOT[5])
+        w5q = quantize_all("w5q", w5_grouped, "gate1_2")
         put(last, idx4, h2[last], gate2)
+        xq_lo = quantize("xq_lo", x_lo[:].rearrange("p c t -> p (c t)"), codes_tile("xq_lo", NP, "gate2_3")[:])
         put(last, idx3, h1[last], gate1)
 
         def passes(acc, second, pair, b, xq, c0):
@@ -341,18 +367,18 @@ def tile_list_crock_slot_scores_kernel(
 
         accs = {}
 
-        def open_chunk(c):
-            for pair in range(2):
-                for second in (1, 0):
-                    acc = bank("acc%d%d%d" % (c, pair, second), 4 * (c % 2) + 2 * pair + second, [P, 2, CH])
-                    accs[(c, pair, second)] = acc
-                    passes(acc, second, pair, 0, xq_lo, CH * c)
+        def open_sum(c, pair, second):
+            acc = bank("acc%d%d%d" % (c, pair, second), 4 * (c % 2) + 2 * pair + second, [P, 2, CH])
+            accs[(c, pair, second)] = acc
+            passes(acc, second, pair, 0, xq_lo, CH * c)
 
         diffs = {}
 
         def close_chunk(c, xq):
             for pair in range(2):
                 for second in (1, 0):
+                    if c >= 2:
+                        open_sum(c, pair, second)
                     passes(accs[(c, pair, second)], second, pair, 1, xq, 0)
                 slot = 2 * (c % 2) + pair
                 size = work_tile("y2abs%d%d" % (c, pair), "size%d" % slot)
@@ -364,7 +390,7 @@ def tile_list_crock_slot_scores_kernel(
         def store_chunk(c):
             for pair in range(2):
                 diff = diffs[(c, pair)]
-                result = raw_tile("result%d%d" % (c, pair), [P, S], F32)
+                result = raw_tile("result%d%d" % (c, pair), [P, S], F32, RESULT_SLOT[(2 * c + pair) % len(RESULT_SLOT)])
                 if 2 * c + pair >= 2 * NCH - ABS_ON_VECTOR:
                     nc.vector.scalar_tensor_tensor(result[:], diff[:], -1.0, diff[:], ALU.mult, ALU.max)
                 else:
@@ -374,8 +400,10 @@ def tile_list_crock_slot_scores_kernel(
                     result[:].rearrange("p (u c) -> p u c", u=2),
                 )
 
-        open_chunk(0)
-        open_chunk(1)
+        for c in range(2):
+            for pair in range(2):
+                for second in (1, 0):
+                    open_sum(c, pair, second)
         xq_hi = []
         picked = picked_tile(last, (last - 1) % 3)
         for c in range(NCH):
@@ -386,11 +414,9 @@ def tile_list_crock_slot_scores_kernel(
                 nc.vector.tensor_scalar(x_hi[c][:, :, PACK - 1], picked[:, cols], gains[:, 1, PACK - 1 : PACK], None, ALU.mult)
             else:
                 nc.scalar.activation(x_hi[c][:, :, PACK - 1], picked[:, cols], ACT.Copy, scale=gains[:, 1, PACK - 1 : PACK])
-            xq_hi.append(quantize("xq_hi%d" % c, x_hi[c][:].rearrange("p c t -> p (c t)"), codes_tile("xq_hi%d" % c, CH)[:]))
+            xq_hi.append(quantize("xq_hi%d" % c, x_hi[c][:].rearrange("p c t -> p (c t)"), codes_tile("xq_hi%d" % c, CH, "minus%d" % c)[:]))
         for c in range(NCH):
             close_chunk(c, xq_hi[c])
-            if c + 2 < NCH:
-                open_chunk(c + 2)
             if c > 0:
                 store_chunk(c - 1)
         store_chunk(NCH - 1)

@@ -23,11 +23,12 @@ KP = P * PACK
 CH = 256
 NCH = NP // CH
 HEAD_SPLIT = 40
-ROUND_ON_VECTOR = (0, 2, 3)
-ABS_ON_VECTOR = 2
+ROUND_ON_VECTOR = (0, 1, 2, 3)
+ABS_ON_VECTOR = 3
 PAGE_SLOT = ["page0", "page1", "page2", "page3", "w3_head", "w1_raw00", "t_words0", "w1_raw10"]
-H2_SLOT = [PAGE_SLOT[i] for i in (2, 3, 4, 6)]
-W5_SLOT = ["t_words1", "w3_tail"]
+VALUE_SLOT = {4: 1, 6: 4}
+PICK_SLOT = [0, 1, 2, 0, 2, 0, 1]
+W5_SLOT = ["t_words1", "w1_raw01"]
 RESULT_SLOT = ["w1_raw01", "w1_raw11", "t_words1", "w3_tail", "w1_raw00", "w3_head", "page1", "page2"]
 
 
@@ -54,8 +55,7 @@ def tile_list_crock_slot_scores_kernel(
             return keep.tile(shape, dtype, name=name, tag=tag or name, align_bytes=64)
 
         def load_scale_rows(plane, scales, q):
-            rows = scales[0, 4 * q : 4 * q + 4, :].bitcast(I32)
-            nc.sync.dma_start(plane[32 * q : 32 * (q + 1), :].bitcast(I32), rows.unsqueeze(0).broadcast_to([8, 4, rows.shape[1]]))
+            nc.sync.dma_start(plane[32 * q : 32 * q + 4, :].bitcast(I32), scales[0, 4 * q : 4 * q + 4, :].bitcast(I32))
 
         def bank(name, index, shape):
             return psum.tile(shape, F32, name=name, tag="bank%d" % index)
@@ -64,6 +64,8 @@ def tile_list_crock_slot_scores_kernel(
         w2_sc_raw = kept("w2_sc_raw", [P, H], U8)
         t_scales = kept("t_scales", [P, T], U8)
         w4_sc = kept("w4_sc", [P, 2, N], U8)
+        nc.vector.memset(t2_scales[:].bitcast(I32), 0)
+        nc.vector.memset(w2_sc_raw[:].bitcast(I32), 0)
         nc.vector.memset(t_scales[:].bitcast(I32), 0)
         nc.vector.memset(w4_sc[:].bitcast(I32), 0)
 
@@ -85,16 +87,15 @@ def tile_list_crock_slot_scores_kernel(
                 nc.tensor.transpose(turned[:, jt, :], rows[:, P * jt : P * (jt + 1)], identity[:])
             return turned
 
-        def deal_gate(name, turned, t, tag):
-            spread = keep.tile([P, PACK, 4, 32], F32, name="%s_spread%d" % (name, t), tag=tag, align_bytes=64)
+        def deal_gate(name, turned, t, spread):
             nc.scalar.activation(
-                spread[:],
+                spread.rearrange("p (jt r q) -> p jt r q", jt=PACK, r=4),
                 turned[:].rearrange("p jt (q t) -> p jt q t", t=PACK)[:, :, :, t].unsqueeze(2).broadcast_to([P, PACK, 4, 32]),
                 ACT.Copy,
             )
             back = bank("%s_back%d" % (name, t), 5 + t % 2, [P, S])
             for jt in range(PACK):
-                nc.tensor.transpose(back[:, P * jt : P * (jt + 1)], spread[:, jt, :, :].rearrange("p r q -> p (r q)"), identity[:])
+                nc.tensor.transpose(back[:, P * jt : P * (jt + 1)], spread[:, P * jt : P * (jt + 1)], identity[:])
             dealt = kept("%s_%d" % (name, t), [P, S], F32)
             nc.scalar.copy(out=dealt[:], in_=back[:])
             return dealt[:]
@@ -106,10 +107,10 @@ def tile_list_crock_slot_scores_kernel(
             pages[i] = keep.tile([P, T2], F32, name="page%d" % i, tag=PAGE_SLOT[i], align_bytes=64)
             nc.sync.dma_start(pages[i][:], page0[KP * b : KP * (b + 1), :].rearrange("(p t) c -> t p c", t=PACK)[t])
 
-        for q in range(4):
-            load_scale_rows(t2_scales, tab2_scales, q)
         wg2_rows = keep.tile([P, S], F32, name="wg2_rows", tag="h1_0", align_bytes=64)
         nc.sync.dma_start(wg2_rows[:], wg2)
+        for q in range(4):
+            load_scale_rows(t2_scales, tab2_scales, q)
         w3_head = load_rows("w3_head", w3, 0, 0, KP)
         w2_lo = kept("w2_lo", [P, 2 * KP], U8)
         nc.sync.dma_start(w2_lo[:].bitcast(I32), w2_words[0, :, 0 : 2 * KP].bitcast(I32))
@@ -131,6 +132,7 @@ def tile_list_crock_slot_scores_kernel(
         for q in range(4):
             nc.sync.dma_start(t_scales[32 * q : 32 * q + 8, :].bitcast(I32), tab_scales[:, 4 * q : 4 * q + 4, :].bitcast(I32))
         load_page(3)
+        idx3 = load_list("idx3", offs3)
         def grouped_tile(name):
             return ring.tile([P, 4 * KP], BF16, name=name, tag="grouped", bufs=3, align_bytes=64)
 
@@ -185,7 +187,7 @@ def tile_list_crock_slot_scores_kernel(
             base = bank("base%d" % i, (i + 2) % 4, [P, S])
             nc.tensor.matmul_mx(out=base[:], lhsT=w2_codes.bitcast(FP4X4), lhsT_scale=w2_plane,
                                 rhs=v2_words[:].bitcast(FP8X4), rhs_scale=v2_scales[:], start=True, stop=True)
-            h2 = work_tile("h2_%d" % i, "h2_%d" % (i % 2))[:]
+            h2 = work_tile("h2_%d" % i, "h2_%d" % i)[:]
             nc.vector.tensor_tensor(h2, base[:], size[:], ALU.subtract)
             return h2
 
@@ -207,18 +209,17 @@ def tile_list_crock_slot_scores_kernel(
                 nc.scalar.activation(sizes[jt][:], side[:], ACT.Abs)
             return list(zip(sizes, minus))
 
-        def stream2_turn_back(i, parts):
+        def stream2_turn_back(i, parts, h2):
             t = i % PACK
             cols = slice(P * t, P * (t + 1))
             total = bank("total%d" % i, i % 2, [P, S])
             for jt in range(PACK):
                 for k in range(2):
                     nc.tensor.matmul(total[:, P * jt : P * (jt + 1)], parts[jt][k][:, cols], identity[:], start=(k == 0), stop=(k == 1), is_transpose=True)
-            h2 = work_tile("h2_%d" % i, H2_SLOT[t])[:]
             nc.scalar.activation(h2, total[:], ACT.Copy, scale=-1.0)
             return h2
 
-        def stream1_values(i, w1q):
+        def stream1_values(i, w1q, h1):
             t = i % PACK
             cols = slice(P * t, P * (t + 1))
             pre = bank("pre%d" % i, 4 + t, [P, S])
@@ -226,7 +227,6 @@ def tile_list_crock_slot_scores_kernel(
                 nc.tensor.matmul_mx(out=pre[:], lhsT=w1q[a][0][:, cols].bitcast(FP8X4), lhsT_scale=w1q[a][1][:, cols],
                                     rhs=v_words[a][:].bitcast(FP8X4), rhs_scale=v_scales[4 * a : P, :],
                                     start=(a == 0), stop=(a == 1))
-            h1 = work_tile("h1_%d" % i, "h1_%d" % t)[:]
             nc.scalar.activation(h1, pre[:], ACT.Gelu_apprx_tanh)
             return h1
 
@@ -258,30 +258,30 @@ def tile_list_crock_slot_scores_kernel(
         v2_words = gather("v2_words", t2_words, idx2, U32)
         v2_scales = gather("v2_scales", t2_scales, idx2, U8)
         grouped = grouped_tile("w3_grouped0")
-        round_dealt(nc.scalar.copy, grouped, w3_head, 0, HEAD_SPLIT)
-        round_dealt(nc.vector.tensor_copy, grouped, w3_head, HEAD_SPLIT, P)
+        round_dealt(nc.vector.tensor_copy, grouped, w3_head, 0, P)
         operands = first_operands("first", grouped, 0, 1) + first_operands("rest", grouped, 1, PACK)
         turned = turn_gate("gate2", wg2_rows)
         h2 = {}
         gate2 = []
+        spread_rest = keep.tile([P, PACK - 1, S], F32, name="spread_rest", tag="w2_lo", align_bytes=64)
+        spreads = [work_tile("spread_first", "spread0")[:]] + [spread_rest[:, u, :] for u in range(PACK - 1)]
         for i in range(PACK):
             h2[i] = stream2_values(i, operands[i])
-            gate2.append(deal_gate("gate2", turned, i, "spread0" if i == 0 else "w2_lo"))
+            gate2.append(deal_gate("gate2", turned, i, spreads[i]))
             if i < PACK - 1:
                 put(i, idx4, h2[i], gate2)
         w1q = quantize_all("w1q_lo", round_w1(0), None)
         turned = turn_gate("gate1", wg1_rows)
-        gate1 = [deal_gate("gate1", turned, t, "spread%d" % (t % 2)) for t in range(PACK)]
+        gate1 = [deal_gate("gate1", turned, t, spreads[t]) for t in range(PACK)]
         v_words = [gather("v_words%d" % a, t_words[a], idx1, U32) for a in range(2)]
         v_scales = gather("v_scales", t_scales, idx1, U8)
-        h1 = {i: stream1_values(i, w1q) for i in range(PACK)}
+        h1 = {i: stream1_values(i, w1q, work_tile("h1_%d" % i, "h1_%d" % i)[:]) for i in range(2)}
         put(PACK - 1, idx4, h2[PACK - 1], gate2)
 
         w3_tail = load_rows("w3_tail", w3, 0, KP, KP)
         w2_hi = kept("w2_hi", [P, 2 * KP], U8)
         nc.sync.dma_start(w2_hi[:].bitcast(I32), w2_words[0, :, 2 * KP : 4 * KP].bitcast(I32))
         w1_raw[(0, 1)] = load_rows("w1_raw01", w1, 0, KP, KP)
-        idx3 = load_list("idx3", offs3)
         w1_raw[(1, 1)] = load_rows("w1_raw11", w1, 1, KP, KP)
         idx5 = load_list("idx5", offs5)
         gains = kept("gains", [P, 2, PACK], F32)
@@ -298,6 +298,9 @@ def tile_list_crock_slot_scores_kernel(
 
         w3_grouped = grouped_tile("w3_grouped1")
         round_dealt(nc.scalar.copy, w3_grouped, w3_tail)
+        h1_pair = keep.tile([P, 2, S], F32, name="h1_pair", tag="w3_tail", align_bytes=64)
+        for i in range(2, PACK):
+            h1[i] = stream1_values(i, w1q, h1_pair[:, i - 2, :])
 
         for i in range(PACK):
             put(i, idx3, h1[i], gate1)
@@ -305,20 +308,50 @@ def tile_list_crock_slot_scores_kernel(
                 parts = stream2_turned(quantize("w3q1", w3_grouped[:], codes_tile("w3q1", KP, "h1_0")[:]))
         w1q = quantize_all("w1q_hi", round_w1(1), None)
 
-        def late_values(i):
-            h2[i] = stream2_turn_back(i, parts)
-            h1[i] = stream1_values(i, w1q)
+        def pair_values(i):
+            first = work_tile("h2_%d" % i, PAGE_SLOT[VALUE_SLOT[i]])
+            both = keep.tile([P, 2, S], F32, name="values%d" % i, tag=PAGE_SLOT[VALUE_SLOT[i] + 1], align_bytes=64)
+            h2[i] = stream2_turn_back(i, parts, first[:])
+            h2[i + 1] = stream2_turn_back(i + 1, parts, both[:, 0, :])
+            h1[i] = stream1_values(i, w1q, both[:, 1, :])
+            h1[i + 1] = stream1_values(i + 1, w1q, work_tile("h1_%d" % (i + 1), "h1_1")[:])
+
+        picked = {}
+
+        def fetch_tile(i):
+            picked[i] = picked_tile(i, PICK_SLOT[i])
+            fetch(i, picked[i], 0, NP)
 
         x_rows = kept("x_rows", [P, PACK, NP], BF16)
-        for i in range(PACK):
-            picked = picked_tile(i, i % 3)
-            fetch(i, picked, 0, NP)
-            if i >= 2:
-                late_values(i + 2)
+
+        def finish_lo(i):
             for c0 in (0, KP):
-                squash(picked, c0, KP)
+                squash(picked[i], c0, KP)
             for c0 in (0, KP):
-                nc.scalar.activation(x_rows[:, i, c0 : c0 + KP], picked[:, c0 : c0 + KP], ACT.Copy, scale=gains[:, 0, i : i + 1])
+                nc.scalar.activation(x_rows[:, i, c0 : c0 + KP], picked[i][:, c0 : c0 + KP], ACT.Copy, scale=gains[:, 0, i : i + 1])
+
+        x_hi = [kept("x_hi%d" % c, [P, CH, PACK], BF16) for c in range(NCH)]
+
+        def finish_hi(i):
+            t = i % PACK
+            for c0 in (0, KP):
+                squash(picked[i], c0, KP)
+            for c in range(NCH):
+                nc.scalar.activation(x_hi[c][:, :, t], picked[i][:, CH * c : CH * (c + 1)], ACT.Copy, scale=gains[:, 1, t : t + 1])
+
+        for i in range(3):
+            fetch_tile(i)
+        finish_lo(0)
+        fetch_tile(3)
+        finish_lo(1)
+        pair_values(4)
+        finish_lo(2)
+        finish_lo(3)
+        for idx, h, gate in ((idx4, h2, gate2), (idx3, h1, gate1)):
+            for i in (4, 5):
+                put(i, idx, h[i], gate)
+        fetch_tile(4)
+        fetch_tile(5)
 
         x_lo = keep.tile([P, NP, PACK], BF16, name="x_lo", tag=PAGE_SLOT[0], align_bytes=64)
         for c in range(NCH):
@@ -326,32 +359,25 @@ def tile_list_crock_slot_scores_kernel(
                 out=x_lo[:, CH * c : CH * (c + 1), :].rearrange("p (c i) t -> p c t i", i=8),
                 in_=x_rows[:, :, CH * c : CH * (c + 1)].rearrange("p t (c i) -> p c t i", i=8),
             )
-        w5_both = keep.tile([P, 2, PACK * N], BF16, name="w5_grouped", tag="x_rows", align_bytes=64)
-        w5_grouped = [w5_both[:, b, :] for b in range(2)]
-
-        x_hi = [kept("x_hi%d" % c, [P, CH, PACK], BF16) for c in range(NCH)]
+        w5_grouped = [grouped_tile("w5_grouped0"), keep.tile([P, PACK * N], BF16, name="w5_grouped1", tag="x_rows", align_bytes=64)]
+        for b in range(2):
+            nc.scalar.copy(
+                out=w5_grouped[b][:].rearrange("p (c i j) -> p c j i", i=4, j=PACK),
+                in_=w5_raw[b][:].rearrange("p j (c i) -> p c j i", i=4),
+            )
+        pair_values(6)
+        finish_hi(4)
+        finish_hi(5)
         last = 2 * PACK - 1
-        for i in range(PACK, last):
-            t = i % PACK
-            put(i, idx4, h2[i], gate2)
-            put(i, idx3, h1[i], gate1)
-            picked = picked_tile(i, i % 3)
-            fetch(i, picked, 0, NP)
-            if i > PACK:
-                late_values(i + 1)
-            for c0 in (0, KP):
-                squash(picked, c0, KP)
-            for c in range(NCH):
-                nc.scalar.activation(x_hi[c][:, :, t], picked[:, CH * c : CH * (c + 1)], ACT.Copy, scale=gains[:, 1, t : t + 1])
-            if t < 2:
-                nc.scalar.copy(
-                    out=w5_grouped[t].rearrange("p (c i j) -> p c j i", i=4, j=PACK),
-                    in_=w5_raw[t][:].rearrange("p j (c i) -> p c j i", i=4),
-                )
-        w5q = quantize_all("w5q", w5_grouped, "gate1_2")
+        put(6, idx4, h2[6], gate2)
         put(last, idx4, h2[last], gate2)
+        put(6, idx3, h1[6], gate1)
         xq_lo = quantize("xq_lo", x_lo[:].rearrange("p c t -> p (c t)"), codes_tile("xq_lo", NP, "gate2_3")[:])
+        fetch_tile(6)
+        finish_hi(6)
+        w5q = [quantize("w5q0", w5_grouped[0][:], codes_tile("w5q0", N, "gate1_2")[:])]
         put(last, idx3, h1[last], gate1)
+        w5q.append(quantize("w5q1", w5_grouped[1][:], codes_tile("w5q1", N, PAGE_SLOT[6])[:]))
 
         def passes(acc, second, pair, b, xq, c0):
             for u in range(2):
@@ -405,15 +431,15 @@ def tile_list_crock_slot_scores_kernel(
                 for second in (1, 0):
                     open_sum(c, pair, second)
         xq_hi = []
-        picked = picked_tile(last, (last - 1) % 3)
+        tail = picked[last - 1]
         for c in range(NCH):
             cols = slice(CH * (c % 2), CH * (c % 2 + 1))
-            nc.vector.tensor_copy(picked[:, cols], pages[last][:].indirect(idx5[:, CH * c // 16 : CH * (c + 1) // 16]))
-            nc.scalar.activation(picked[:, cols], picked[:, cols], ACT.Tanh)
+            nc.vector.tensor_copy(tail[:, cols], pages[last][:].indirect(idx5[:, CH * c // 16 : CH * (c + 1) // 16]))
+            nc.scalar.activation(tail[:, cols], tail[:, cols], ACT.Tanh)
             if c in ROUND_ON_VECTOR:
-                nc.vector.tensor_scalar(x_hi[c][:, :, PACK - 1], picked[:, cols], gains[:, 1, PACK - 1 : PACK], None, ALU.mult)
+                nc.vector.tensor_scalar(x_hi[c][:, :, PACK - 1], tail[:, cols], gains[:, 1, PACK - 1 : PACK], None, ALU.mult)
             else:
-                nc.scalar.activation(x_hi[c][:, :, PACK - 1], picked[:, cols], ACT.Copy, scale=gains[:, 1, PACK - 1 : PACK])
+                nc.scalar.activation(x_hi[c][:, :, PACK - 1], tail[:, cols], ACT.Copy, scale=gains[:, 1, PACK - 1 : PACK])
             xq_hi.append(quantize("xq_hi%d" % c, x_hi[c][:].rearrange("p c t -> p (c t)"), codes_tile("xq_hi%d" % c, CH, "minus%d" % c)[:]))
         for c in range(NCH):
             close_chunk(c, xq_hi[c])

@@ -20,16 +20,15 @@ ALU = mybir.AluOpType
 P = 128
 PACK = 4
 KP = P * PACK
+QUADS = 4
+LAST = 2 * PACK - 1
 CH = 256
 NCH = NP // CH
-HEAD_SPLIT = 40
-ROUND_ON_VECTOR = (0, 1, 2, 3)
-ABS_ON_VECTOR = 3
-PAGE_SLOT = ["page0", "page1", "page2", "page3", "w3_head", "w1_raw00", "t_words0", "w1_raw10"]
-VALUE_SLOT = {4: 1, 6: 4}
-PICK_SLOT = [0, 1, 2, 0, 2, 0, 1]
-W5_SLOT = ["t_words1", "w1_raw01"]
-RESULT_SLOT = ["w1_raw01", "w1_raw11", "t_words1", "w3_tail", "w1_raw00", "w3_head", "page1", "page2"]
+
+PAGE_TAG = ["page0", "page1", "page2", "page3", "w3_lo", "w1_raw00", "t_words0", "w1_raw10"]
+W5_TAG = ["t_words1", "w1_raw01"]
+RESULT_TAG = ["w1_raw01", "w1_raw11", "t_words1", "w3_hi", "w1_raw00", "w3_lo", "page1", "page2"]
+PICKED_TAG = ["picked0", "picked1", "picked2", "picked0", "picked2", "picked0", "picked1"]
 
 
 def tile_list_crock_slot_scores_kernel(
@@ -40,344 +39,328 @@ def tile_list_crock_slot_scores_kernel(
     with ExitStack() as ctx:
         lists = ctx.enter_context(tc.tile_pool(name="lists", bufs=1))
         keep = ctx.enter_context(tc.tile_pool(name="keep", bufs=1))
-        ring = ctx.enter_context(tc.tile_pool(name="ring", bufs=1))
+        ring = ctx.enter_context(tc.tile_pool(name="ring", bufs=3))
         psum = ctx.enter_context(tc.psum_pool(name="psum", bufs=1))
 
-        def kept(name, shape, dtype):
-            return keep.tile(shape, dtype, name=name, align_bytes=64)
+        def sbuf(name, shape, dtype, tag=None):
+            return keep.tile(shape, dtype, name=name, tag=tag or name, align_bytes=64)
+
+        def values(name, tag):
+            return sbuf(name, [P, S], F32, tag)
+
+        def bank(name, index):
+            return psum.tile([P, S], F32, name=name, tag="bank%d" % index)
+
+        def rounded_tile(name):
+            return ring.tile([P, PACK * KP], BF16, name=name, tag="rounded", align_bytes=64)
 
         def load_list(name, src):
             tile = lists.tile(list(src.shape), U16, name=name)
             nc.sync.dma_start(tile[:], src)
             return tile
 
-        def raw_tile(name, shape, dtype, tag=None):
-            return keep.tile(shape, dtype, name=name, tag=tag or name, align_bytes=64)
+        def load_bytes(tile_ap, src):
+            nc.sync.dma_start(tile_ap.bitcast(I32), src.bitcast(I32))
 
-        def load_scale_rows(plane, scales, q):
-            nc.sync.dma_start(plane[32 * q : 32 * q + 4, :].bitcast(I32), scales[0, 4 * q : 4 * q + 4, :].bitcast(I32))
-
-        def bank(name, index, shape):
-            return psum.tile(shape, F32, name=name, tag="bank%d" % index)
-
-        t2_scales = kept("t2_scales", [P, TB], U8)
-        w2_sc_raw = kept("w2_sc_raw", [P, H], U8)
-        t_scales = kept("t_scales", [P, T], U8)
-        w4_sc = kept("w4_sc", [P, 2, N], U8)
-        nc.vector.memset(t2_scales[:].bitcast(I32), 0)
-        nc.vector.memset(w2_sc_raw[:].bitcast(I32), 0)
-        nc.vector.memset(t_scales[:].bitcast(I32), 0)
-        nc.vector.memset(w4_sc[:].bitcast(I32), 0)
-
-        t2_words = kept("t2_words", [P, TB], U32)
-        nc.sync.dma_start(t2_words[:].bitcast(I32), tab2_words[0].rearrange("p n i -> p (n i)").bitcast(I32))
-        idx2 = load_list("idx2", offs2)
-
-        def load_rows(name, w, a, c0, width, tag=None):
-            raw = raw_tile(name, [P, PACK, width], F32, tag)
-            nc.sync.dma_start(raw[:], w[KP * a : KP * (a + 1), c0 : c0 + width].rearrange("(p j) c -> p j c", j=PACK))
+        def load_rows(name, w, a, c0, tag=None):
+            raw = sbuf(name, [P, PACK, KP], F32, tag)
+            nc.sync.dma_start(raw[:], w[KP * a : KP * (a + 1), c0 : c0 + KP].rearrange("(p j) c -> p j c", j=PACK))
             return raw
 
-        identity = kept("identity", [P, P], F32)
-        make_identity(nc, identity[:])
-
-        def turn_gate(name, rows):
-            turned = bank(name + "_turned", 4, [P, PACK, P])
-            for jt in range(PACK):
-                nc.tensor.transpose(turned[:, jt, :], rows[:, P * jt : P * (jt + 1)], identity[:])
-            return turned
-
-        def deal_gate(name, turned, t, spread):
-            nc.scalar.activation(
-                spread.rearrange("p (jt r q) -> p jt r q", jt=PACK, r=4),
-                turned[:].rearrange("p jt (q t) -> p jt q t", t=PACK)[:, :, :, t].unsqueeze(2).broadcast_to([P, PACK, 4, 32]),
-                ACT.Copy,
-            )
-            back = bank("%s_back%d" % (name, t), 5 + t % 2, [P, S])
-            for jt in range(PACK):
-                nc.tensor.transpose(back[:, P * jt : P * (jt + 1)], spread[:, P * jt : P * (jt + 1)], identity[:])
-            dealt = kept("%s_%d" % (name, t), [P, S], F32)
-            nc.scalar.copy(out=dealt[:], in_=back[:])
-            return dealt[:]
+        def load_gate(name, wg, tag):
+            rows = values(name, tag)
+            nc.sync.dma_start(rows[:], wg)
+            return rows
 
         pages = {}
 
         def load_page(i):
             b, t = divmod(i, PACK)
-            pages[i] = keep.tile([P, T2], F32, name="page%d" % i, tag=PAGE_SLOT[i], align_bytes=64)
+            pages[i] = sbuf("page%d" % i, [P, T2], F32, PAGE_TAG[i])
             nc.sync.dma_start(pages[i][:], page0[KP * b : KP * (b + 1), :].rearrange("(p t) c -> t p c", t=PACK)[t])
 
-        wg2_rows = keep.tile([P, S], F32, name="wg2_rows", tag="h1_0", align_bytes=64)
-        nc.sync.dma_start(wg2_rows[:], wg2)
-        for q in range(4):
-            load_scale_rows(t2_scales, tab2_scales, q)
-        w3_head = load_rows("w3_head", w3, 0, 0, KP)
-        w2_lo = kept("w2_lo", [P, 2 * KP], U8)
-        nc.sync.dma_start(w2_lo[:].bitcast(I32), w2_words[0, :, 0 : 2 * KP].bitcast(I32))
-        for q in range(4):
-            load_scale_rows(w2_sc_raw, w2_scales, q)
+        t2_plane = sbuf("t2_plane", [P, TB], U8)
+        w2_plane = sbuf("w2_plane", [P, H], U8)
+        t_plane = sbuf("t_plane", [P, T], U8)
+        w4_plane = sbuf("w4_plane", [P, 2, N], U8)
+        for plane in (t2_plane, w2_plane, t_plane, w4_plane):
+            nc.vector.memset(plane[:].bitcast(I32), 0)
+
+        identity = sbuf("identity", [P, P], F32)
+        make_identity(nc, identity[:])
+
+        t2_words = sbuf("t2_words", [P, TB], U32)
+        load_bytes(t2_words[:], tab2_words[0].rearrange("p n i -> p (n i)"))
+        idx2 = load_list("idx2", offs2)
+        wg2_rows = load_gate("wg2_rows", wg2, "h1_0")
+        for q in range(QUADS):
+            load_bytes(t2_plane[32 * q : 32 * q + 4, :], tab2_scales[0, 4 * q : 4 * q + 4, :])
+        w3_lo = load_rows("w3_lo", w3, 0, 0)
+        w2_lo = sbuf("w2_lo", [P, 2 * KP], U8)
+        load_bytes(w2_lo[:], w2_words[0, :, 0 : 2 * KP])
+        for q in range(QUADS):
+            load_bytes(w2_plane[32 * q : 32 * q + 4, :], w2_scales[0, 4 * q : 4 * q + 4, :])
         load_page(0)
         idx4 = load_list("idx4", offs4)
         load_page(1)
         load_page(2)
-        w1_raw = {(a, 0): load_rows("w1_raw%d0" % a, w1, a, 0, KP) for a in range(2)}
-        wg1_rows = keep.tile([P, S], F32, name="wg1_rows", tag="h1_1", align_bytes=64)
-        nc.sync.dma_start(wg1_rows[:], wg1)
+        w1_raw = {(a, 0): load_rows("w1_raw%d0" % a, w1, a, 0) for a in range(2)}
+        wg1_rows = load_gate("wg1_rows", wg1, "h1_1")
         idx1 = load_list("idx1", offs)
         t_words = []
         for a in range(2):
-            words = raw_tile("t_words%d" % a, [P, T], U32)
-            nc.sync.dma_start(words[:].bitcast(I32), tab_words[a].rearrange("p n i -> p (n i)").bitcast(I32))
-            t_words.append(words)
-        for q in range(4):
-            nc.sync.dma_start(t_scales[32 * q : 32 * q + 8, :].bitcast(I32), tab_scales[:, 4 * q : 4 * q + 4, :].bitcast(I32))
+            t_words.append(sbuf("t_words%d" % a, [P, T], U32))
+            load_bytes(t_words[a][:], tab_words[a].rearrange("p n i -> p (n i)"))
+        for q in range(QUADS):
+            load_bytes(t_plane[32 * q : 32 * q + 8, :], tab_scales[:, 4 * q : 4 * q + 4, :])
         load_page(3)
         idx3 = load_list("idx3", offs3)
-        def grouped_tile(name):
-            return ring.tile([P, 4 * KP], BF16, name=name, tag="grouped", bufs=3, align_bytes=64)
 
-        def round_dealt(copy, grouped, raw, m0=0, m1=P):
+        def round_dealt(copy, raw, name):
+            rounded = rounded_tile(name)
             copy(
-                out=grouped[:].rearrange("p (t m j) -> p m j t", t=PACK, j=PACK)[:, m0:m1, :, :],
-                in_=raw[:].rearrange("p j (m t) -> p m j t", t=PACK)[:, m0:m1, :, :],
+                out=rounded[:].rearrange("p (t m j) -> p m j t", t=PACK, j=PACK),
+                in_=raw[:].rearrange("p j (m t) -> p m j t", t=PACK),
             )
+            return rounded
 
         def quantize(name, src, codes):
-            scales = kept(name + "_scales", [P, codes.shape[1]], U8)
-            nc.vector.quantize_mx(out=codes.bitcast(FP8X4), scales=scales[:], in_=src)
-            return codes, scales
+            plane = sbuf(name + "_plane", [P, codes.shape[1]], U8)
+            nc.vector.quantize_mx(out=codes.bitcast(FP8X4), scales=plane[:], in_=src)
+            return codes, plane
 
-        def codes_tile(name, width, tag=None):
-            return keep.tile([P, width], U32, name=name, tag=tag or name, align_bytes=64)
+        def quantize_passes(name, rounded, tag=None):
+            codes = sbuf(name, [P, len(rounded) * KP], U32, tag)
+            return [quantize("%s%d" % (name, a), src[:], codes[:, KP * a : KP * (a + 1)]) for a, src in enumerate(rounded)]
 
-        def gather(name, window, idx, dtype):
-            tile = kept(name, [P, S], dtype)
+        def gather_table(name, window, idx, dtype):
+            tile = sbuf(name, [P, S], dtype)
             nc.vector.tensor_copy(tile[:], window[:].indirect(idx[:]))
             return tile
 
-        def first_operands(name, grouped, t0, t1):
+        def stream2_operands(name, w3_rounded, t0, t1):
             count = t1 - t0
-            w3q = quantize("w3q_" + name, grouped[:, KP * t0 : KP * t1], codes_tile("w3q_" + name, P * count)[:])
-            words = kept("w2_dealt_" + name, [P, 2 * P * count], U8)
-            scales = kept("w2_sc_" + name, [P, P * count], U8)
+            w3q = quantize("w3q_" + name, w3_rounded[:, KP * t0 : KP * t1], sbuf("w3q_" + name, [P, P * count], U32)[:])
+            words = sbuf("w2_dealt_" + name, [P, 2 * P * count], U8)
+            plane = sbuf("w2_plane_dealt_" + name, [P, P * count], U8)
             nc.vector.tensor_copy(
                 out=words[:].rearrange("p (t m e) -> p m t e", t=count, e=2),
                 in_=w2_lo[:].rearrange("p (m t e) -> p m t e", t=PACK, e=2)[:, :, t0:t1, :],
             )
             nc.vector.tensor_copy(
-                out=scales[:].rearrange("p (t m) -> p m t", t=count),
-                in_=w2_sc_raw[:, 0:KP].rearrange("p (m t) -> p m t", t=PACK)[:, :, t0:t1],
+                out=plane[:].rearrange("p (t m) -> p m t", t=count),
+                in_=w2_plane[:, 0:KP].rearrange("p (m t) -> p m t", t=PACK)[:, :, t0:t1],
             )
             return [
                 (w3q[0][:, P * u : P * (u + 1)], w3q[1][:, P * u : P * (u + 1)],
-                 words[:, 2 * P * u : 2 * P * (u + 1)], scales[:, P * u : P * (u + 1)])
+                 words[:, 2 * P * u : 2 * P * (u + 1)], plane[:, P * u : P * (u + 1)])
                 for u in range(count)
             ]
 
-        def work_tile(name, tag):
-            return keep.tile([P, S], F32, name=name, tag=tag, align_bytes=64)
+        def turn_gate(name, rows):
+            turned = bank(name + "_turned", 4)
+            for jt in range(S // P):
+                nc.tensor.transpose(turned[:, P * jt : P * (jt + 1)], rows[:, P * jt : P * (jt + 1)], identity[:])
+            return turned
 
-        def stream2_values(i, operands):
-            w3_codes, w3_scales, w2_codes, w2_plane = operands
-            side = bank("side%d" % i, i % 2, [P, S])
-            nc.tensor.matmul_mx(out=side[:], lhsT=w3_codes.bitcast(FP8X4), lhsT_scale=w3_scales,
-                                rhs=v2_words[:].bitcast(FP8X4), rhs_scale=v2_scales[:], start=True, stop=True)
-            size = work_tile("size%d" % i, "size%d" % i)
+        def deal_gate(name, turned, t, spread):
+            picked_rows = turned[:].rearrange("p (jt q t) -> p jt q t", jt=S // P, t=PACK)[:, :, :, t]
+            nc.scalar.activation(
+                spread.rearrange("p (jt r q) -> p jt r q", jt=S // P, r=QUADS),
+                picked_rows.unsqueeze(2).broadcast_to([P, S // P, QUADS, 32]),
+                ACT.Copy,
+            )
+            back = bank("%s_back%d" % (name, t), 5 + t % 2)
+            for jt in range(S // P):
+                nc.tensor.transpose(back[:, P * jt : P * (jt + 1)], spread[:, P * jt : P * (jt + 1)], identity[:])
+            dealt = sbuf("%s_%d" % (name, t), [P, S], F32)
+            nc.scalar.copy(out=dealt[:], in_=back[:])
+            return dealt[:]
+
+        def stream2_direct(i, operands):
+            w3_codes, w3_plane, w2_codes, w2_dealt_plane = operands
+            side = bank("side%d" % i, i % 2)
+            nc.tensor.matmul_mx(out=side[:], lhsT=w3_codes.bitcast(FP8X4), lhsT_scale=w3_plane,
+                                rhs=v2_words[:].bitcast(FP8X4), rhs_scale=v2_plane[:], start=True, stop=True)
+            size = values("size%d" % i, "size%d" % i)
             nc.scalar.activation(size[:], side[:], ACT.Abs)
-            base = bank("base%d" % i, (i + 2) % 4, [P, S])
-            nc.tensor.matmul_mx(out=base[:], lhsT=w2_codes.bitcast(FP4X4), lhsT_scale=w2_plane,
-                                rhs=v2_words[:].bitcast(FP8X4), rhs_scale=v2_scales[:], start=True, stop=True)
-            h2 = work_tile("h2_%d" % i, "h2_%d" % i)[:]
-            nc.vector.tensor_tensor(h2, base[:], size[:], ALU.subtract)
-            return h2
+            base = bank("base%d" % i, (i + 2) % 4)
+            nc.tensor.matmul_mx(out=base[:], lhsT=w2_codes.bitcast(FP4X4), lhsT_scale=w2_dealt_plane,
+                                rhs=v2_words[:].bitcast(FP8X4), rhs_scale=v2_plane[:], start=True, stop=True)
+            result = values("h2_%d" % i, "h2_%d" % i)[:]
+            nc.vector.tensor_tensor(result, base[:], size[:], ALU.subtract)
+            return result
 
         def stream2_turned(w3q):
             minus, sizes = [], []
-            for jt in range(PACK):
+            for jt in range(S // P):
                 entries = slice(P * jt, P * (jt + 1))
-                base = bank("base_turned%d" % jt, jt, [P, KP])
-                nc.tensor.matmul_mx(out=base[:], lhsT=v2_words[:, entries].bitcast(FP8X4), lhsT_scale=v2_scales[:, entries],
-                                    rhs=w2_hi[:].bitcast(FP4X4), rhs_scale=w2_sc_raw[:, KP : 2 * KP], start=True, stop=True)
-                minus.append(work_tile("minus_base%d" % jt, "minus%d" % jt))
-                nc.scalar.activation(minus[jt][:].rearrange("p (t m) -> p t m", t=PACK), base[:].rearrange("p (m t) -> p t m", t=PACK), ACT.Copy, scale=-1.0)
-            for jt in range(PACK):
+                base = bank("base_turned%d" % jt, jt)
+                nc.tensor.matmul_mx(out=base[:], lhsT=v2_words[:, entries].bitcast(FP8X4), lhsT_scale=v2_plane[:, entries],
+                                    rhs=w2_hi[:].bitcast(FP4X4), rhs_scale=w2_plane[:, KP : 2 * KP], start=True, stop=True)
+                minus.append(values("minus_base%d" % jt, "minus%d" % jt))
+                nc.scalar.activation(
+                    minus[jt][:].rearrange("p (t m) -> p t m", t=PACK),
+                    base[:].rearrange("p (m t) -> p t m", t=PACK), ACT.Copy, scale=-1.0,
+                )
+            for jt in range(S // P):
                 entries = slice(P * jt, P * (jt + 1))
-                side = bank("side_turned%d" % jt, jt, [P, KP])
-                nc.tensor.matmul_mx(out=side[:], lhsT=v2_words[:, entries].bitcast(FP8X4), lhsT_scale=v2_scales[:, entries],
+                side = bank("side_turned%d" % jt, jt)
+                nc.tensor.matmul_mx(out=side[:], lhsT=v2_words[:, entries].bitcast(FP8X4), lhsT_scale=v2_plane[:, entries],
                                     rhs=w3q[0].bitcast(FP8X4), rhs_scale=w3q[1][:], start=True, stop=True)
-                sizes.append(work_tile("size_turned%d" % jt, "size%d" % jt))
+                sizes.append(values("size_turned%d" % jt, "size%d" % jt))
                 nc.scalar.activation(sizes[jt][:], side[:], ACT.Abs)
             return list(zip(sizes, minus))
 
-        def stream2_turn_back(i, parts, h2):
-            t = i % PACK
-            cols = slice(P * t, P * (t + 1))
-            total = bank("total%d" % i, i % 2, [P, S])
-            for jt in range(PACK):
+        def stream2_turn_back(i, parts, result):
+            cols = slice(P * (i % PACK), P * (i % PACK + 1))
+            total = bank("total%d" % i, i % 2)
+            for jt in range(S // P):
                 for k in range(2):
-                    nc.tensor.matmul(total[:, P * jt : P * (jt + 1)], parts[jt][k][:, cols], identity[:], start=(k == 0), stop=(k == 1), is_transpose=True)
-            nc.scalar.activation(h2, total[:], ACT.Copy, scale=-1.0)
-            return h2
-
-        def stream1_values(i, w1q, h1):
-            t = i % PACK
-            cols = slice(P * t, P * (t + 1))
-            pre = bank("pre%d" % i, 4 + t, [P, S])
-            for a in range(2):
-                nc.tensor.matmul_mx(out=pre[:], lhsT=w1q[a][0][:, cols].bitcast(FP8X4), lhsT_scale=w1q[a][1][:, cols],
-                                    rhs=v_words[a][:].bitcast(FP8X4), rhs_scale=v_scales[4 * a : P, :],
-                                    start=(a == 0), stop=(a == 1))
-            nc.scalar.activation(h1, pre[:], ACT.Gelu_apprx_tanh)
-            return h1
-
-        def put(i, idx, values, gate):
-            nc.vector.tensor_tensor(pages[i][:].indirect(idx[:]), values, gate[i % PACK], ALU.mult)
-
-        def picked_tile(i, slot):
-            return keep.tile([P, NP], F32, name="picked%d" % i, tag="picked%d" % slot)
-
-        def fetch(i, picked, c0, width):
-            cols = slice(c0, c0 + width)
-            nc.vector.tensor_copy(picked[:, cols], pages[i][:].indirect(idx5[:, c0 // 16 : (c0 + width) // 16]))
-
-        def squash(picked, c0, width):
-            nc.scalar.activation(picked[:, c0 : c0 + width], picked[:, c0 : c0 + width], ACT.Tanh)
-
-        def round_w1(b):
-            result = []
-            for a in range(2):
-                grouped = grouped_tile("w1_grouped%d%d" % (a, b))
-                round_dealt(nc.scalar.copy, grouped, w1_raw[(a, b)])
-                result.append(grouped[:])
+                    nc.tensor.matmul(total[:, P * jt : P * (jt + 1)], parts[jt][k][:, cols], identity[:],
+                                     start=(k == 0), stop=(k == 1), is_transpose=True)
+            nc.scalar.activation(result, total[:], ACT.Copy, scale=-1.0)
             return result
 
-        def quantize_all(name, grouped, tag):
-            codes = codes_tile(name, len(grouped) * KP, tag)
-            return [quantize("%s%d" % (name, a), src, codes[:, KP * a : KP * (a + 1)]) for a, src in enumerate(grouped)]
+        def stream1(i, w1q, result):
+            cols = slice(P * (i % PACK), P * (i % PACK + 1))
+            pre = bank("pre%d" % i, 4 + i % PACK)
+            for a in range(2):
+                nc.tensor.matmul_mx(out=pre[:], lhsT=w1q[a][0][:, cols].bitcast(FP8X4), lhsT_scale=w1q[a][1][:, cols],
+                                    rhs=v_words[a][:].bitcast(FP8X4), rhs_scale=v_plane[4 * a : P, :],
+                                    start=(a == 0), stop=(a == 1))
+            nc.scalar.activation(result, pre[:], ACT.Gelu_apprx_tanh)
+            return result
 
-        v2_words = gather("v2_words", t2_words, idx2, U32)
-        v2_scales = gather("v2_scales", t2_scales, idx2, U8)
-        grouped = grouped_tile("w3_grouped0")
-        round_dealt(nc.vector.tensor_copy, grouped, w3_head, 0, P)
-        operands = first_operands("first", grouped, 0, 1) + first_operands("rest", grouped, 1, PACK)
+        h1, h2 = {}, {}
+
+        def put1(i):
+            nc.vector.tensor_tensor(pages[i][:].indirect(idx3[:]), h1[i], gate1[i % PACK], ALU.mult)
+
+        def put2(i):
+            nc.vector.tensor_tensor(pages[i][:].indirect(idx4[:]), h2[i], gate2[i % PACK], ALU.mult)
+
+        v2_words = gather_table("v2_words", t2_words, idx2, U32)
+        v2_plane = gather_table("v2_plane", t2_plane, idx2, U8)
+        w3_rounded = round_dealt(nc.vector.tensor_copy, w3_lo, "w3_rounded_lo")
+        operands = stream2_operands("first", w3_rounded, 0, 1) + stream2_operands("rest", w3_rounded, 1, PACK)
         turned = turn_gate("gate2", wg2_rows)
-        h2 = {}
+        spread_rest = sbuf("spread_rest", [P, PACK - 1, S], F32, "w2_lo")
+        spreads = [values("spread_first", "spread_first")[:]] + [spread_rest[:, u, :] for u in range(PACK - 1)]
         gate2 = []
-        spread_rest = keep.tile([P, PACK - 1, S], F32, name="spread_rest", tag="w2_lo", align_bytes=64)
-        spreads = [work_tile("spread_first", "spread0")[:]] + [spread_rest[:, u, :] for u in range(PACK - 1)]
         for i in range(PACK):
-            h2[i] = stream2_values(i, operands[i])
+            h2[i] = stream2_direct(i, operands[i])
             gate2.append(deal_gate("gate2", turned, i, spreads[i]))
             if i < PACK - 1:
-                put(i, idx4, h2[i], gate2)
-        w1q = quantize_all("w1q_lo", round_w1(0), None)
+                put2(i)
+        w1q = quantize_passes("w1q_lo", [round_dealt(nc.scalar.copy, w1_raw[(a, 0)], "w1_rounded%d0" % a) for a in range(2)])
         turned = turn_gate("gate1", wg1_rows)
         gate1 = [deal_gate("gate1", turned, t, spreads[t]) for t in range(PACK)]
-        v_words = [gather("v_words%d" % a, t_words[a], idx1, U32) for a in range(2)]
-        v_scales = gather("v_scales", t_scales, idx1, U8)
-        h1 = {i: stream1_values(i, w1q, work_tile("h1_%d" % i, "h1_%d" % i)[:]) for i in range(2)}
-        put(PACK - 1, idx4, h2[PACK - 1], gate2)
+        v_words = [gather_table("v_words%d" % a, t_words[a], idx1, U32) for a in range(2)]
+        v_plane = gather_table("v_plane", t_plane, idx1, U8)
+        for i in range(2):
+            h1[i] = stream1(i, w1q, values("h1_%d" % i, "h1_%d" % i)[:])
+        put2(PACK - 1)
 
-        w3_tail = load_rows("w3_tail", w3, 0, KP, KP)
-        w2_hi = kept("w2_hi", [P, 2 * KP], U8)
-        nc.sync.dma_start(w2_hi[:].bitcast(I32), w2_words[0, :, 2 * KP : 4 * KP].bitcast(I32))
-        w1_raw[(0, 1)] = load_rows("w1_raw01", w1, 0, KP, KP)
-        w1_raw[(1, 1)] = load_rows("w1_raw11", w1, 1, KP, KP)
+        w3_hi = load_rows("w3_hi", w3, 0, KP)
+        w2_hi = sbuf("w2_hi", [P, 2 * KP], U8)
+        load_bytes(w2_hi[:], w2_words[0, :, 2 * KP : 4 * KP])
+        for a in range(2):
+            w1_raw[(a, 1)] = load_rows("w1_raw%d1" % a, w1, a, KP)
         idx5 = load_list("idx5", offs5)
-        gains = kept("gains", [P, 2, PACK], F32)
+        gains = sbuf("gains", [P, 2, PACK], F32)
         nc.sync.dma_start(gains[:], gain.rearrange("(b p t) -> p b t", p=P, t=PACK))
-        for i in range(PACK, 2 * PACK - 1):
+        for i in range(PACK, LAST):
             load_page(i)
-        w4_w = kept("w4_w", [P, 2, 2 * N], U8)
-        nc.sync.dma_start(w4_w[:].bitcast(I32), w4_words.rearrange("a p n -> p a n").bitcast(I32))
-        for q in range(4):
-            nc.sync.dma_start(w4_sc[32 * q : 32 * q + 4, :, :].bitcast(I32),
-                              w4_scales[:, 4 * q : 4 * q + 4, :].rearrange("a q n -> q a n").bitcast(I32))
-        w5_raw = [load_rows("w5_raw%d" % b, w5, b, 0, N, W5_SLOT[b]) for b in range(2)]
-        load_page(7)
+        w4_w = sbuf("w4_w", [P, 2, 2 * N], U8)
+        load_bytes(w4_w[:], w4_words.rearrange("a p n -> p a n"))
+        for q in range(QUADS):
+            load_bytes(w4_plane[32 * q : 32 * q + 4, :, :], w4_scales[:, 4 * q : 4 * q + 4, :].rearrange("a q n -> q a n"))
+        w5_raw = [load_rows("w5_raw%d" % b, w5, b, 0, W5_TAG[b]) for b in range(2)]
+        load_page(LAST)
 
-        w3_grouped = grouped_tile("w3_grouped1")
-        round_dealt(nc.scalar.copy, w3_grouped, w3_tail)
-        h1_pair = keep.tile([P, 2, S], F32, name="h1_pair", tag="w3_tail", align_bytes=64)
+        w3_rounded = round_dealt(nc.scalar.copy, w3_hi, "w3_rounded_hi")
+        h1_pair = sbuf("h1_pair", [P, 2, S], F32, "w3_hi")
         for i in range(2, PACK):
-            h1[i] = stream1_values(i, w1q, h1_pair[:, i - 2, :])
-
+            h1[i] = stream1(i, w1q, h1_pair[:, i - 2, :])
         for i in range(PACK):
-            put(i, idx3, h1[i], gate1)
+            put1(i)
             if i == 0:
-                parts = stream2_turned(quantize("w3q1", w3_grouped[:], codes_tile("w3q1", KP, "h1_0")[:]))
-        w1q = quantize_all("w1q_hi", round_w1(1), None)
+                parts = stream2_turned(quantize("w3q_hi", w3_rounded[:], sbuf("w3q_hi", [P, KP], U32, "h1_0")[:]))
+        w1q = quantize_passes("w1q_hi", [round_dealt(nc.scalar.copy, w1_raw[(a, 1)], "w1_rounded%d1" % a) for a in range(2)])
 
-        def pair_values(i):
-            first = work_tile("h2_%d" % i, PAGE_SLOT[VALUE_SLOT[i]])
-            both = keep.tile([P, 2, S], F32, name="values%d" % i, tag=PAGE_SLOT[VALUE_SLOT[i] + 1], align_bytes=64)
+        def pair_values(i, freed):
+            first = values("h2_%d" % i, PAGE_TAG[freed])
+            both = sbuf("values%d" % i, [P, 2, S], F32, PAGE_TAG[freed + 1])
             h2[i] = stream2_turn_back(i, parts, first[:])
             h2[i + 1] = stream2_turn_back(i + 1, parts, both[:, 0, :])
-            h1[i] = stream1_values(i, w1q, both[:, 1, :])
-            h1[i + 1] = stream1_values(i + 1, w1q, work_tile("h1_%d" % (i + 1), "h1_1")[:])
+            h1[i] = stream1(i, w1q, both[:, 1, :])
+            h1[i + 1] = stream1(i + 1, w1q, values("h1_%d" % (i + 1), "h1_1")[:])
 
         picked = {}
 
-        def fetch_tile(i):
-            picked[i] = picked_tile(i, PICK_SLOT[i])
-            fetch(i, picked[i], 0, NP)
+        def fetch(i):
+            picked[i] = sbuf("picked_from%d" % i, [P, NP], F32, PICKED_TAG[i])
+            nc.vector.tensor_copy(picked[i][:], pages[i][:].indirect(idx5[:]))
 
-        x_rows = kept("x_rows", [P, PACK, NP], BF16)
+        def squash(i):
+            for c0 in (0, NP // 2):
+                half = picked[i][:, c0 : c0 + NP // 2]
+                nc.scalar.activation(half, half, ACT.Tanh)
+
+        x_rows = sbuf("x_rows", [P, PACK, NP], BF16)
 
         def finish_lo(i):
-            for c0 in (0, KP):
-                squash(picked[i], c0, KP)
-            for c0 in (0, KP):
-                nc.scalar.activation(x_rows[:, i, c0 : c0 + KP], picked[i][:, c0 : c0 + KP], ACT.Copy, scale=gains[:, 0, i : i + 1])
+            squash(i)
+            for c0 in (0, NP // 2):
+                cols = slice(c0, c0 + NP // 2)
+                nc.scalar.activation(x_rows[:, i, cols], picked[i][:, cols], ACT.Copy, scale=gains[:, 0, i : i + 1])
 
-        x_hi = [kept("x_hi%d" % c, [P, CH, PACK], BF16) for c in range(NCH)]
+        x_hi = [sbuf("x_hi%d" % c, [P, CH, PACK], BF16) for c in range(NCH)]
 
         def finish_hi(i):
             t = i % PACK
-            for c0 in (0, KP):
-                squash(picked[i], c0, KP)
+            squash(i)
             for c in range(NCH):
                 nc.scalar.activation(x_hi[c][:, :, t], picked[i][:, CH * c : CH * (c + 1)], ACT.Copy, scale=gains[:, 1, t : t + 1])
 
         for i in range(3):
-            fetch_tile(i)
+            fetch(i)
         finish_lo(0)
-        fetch_tile(3)
+        fetch(3)
         finish_lo(1)
-        pair_values(4)
+        pair_values(4, freed=1)
         finish_lo(2)
         finish_lo(3)
-        for idx, h, gate in ((idx4, h2, gate2), (idx3, h1, gate1)):
+        for put in (put2, put1):
             for i in (4, 5):
-                put(i, idx, h[i], gate)
-        fetch_tile(4)
-        fetch_tile(5)
+                put(i)
+        fetch(4)
+        fetch(5)
 
-        x_lo = keep.tile([P, NP, PACK], BF16, name="x_lo", tag=PAGE_SLOT[0], align_bytes=64)
+        x_lo = sbuf("x_lo", [P, NP, PACK], BF16, PAGE_TAG[0])
         for c in range(NCH):
             nc.scalar.copy(
                 out=x_lo[:, CH * c : CH * (c + 1), :].rearrange("p (c i) t -> p c t i", i=8),
                 in_=x_rows[:, :, CH * c : CH * (c + 1)].rearrange("p t (c i) -> p c t i", i=8),
             )
-        w5_grouped = [grouped_tile("w5_grouped0"), keep.tile([P, PACK * N], BF16, name="w5_grouped1", tag="x_rows", align_bytes=64)]
+        w5_rounded = [rounded_tile("w5_rounded0"), sbuf("w5_rounded1", [P, PACK * N], BF16, "x_rows")]
         for b in range(2):
             nc.scalar.copy(
-                out=w5_grouped[b][:].rearrange("p (c i j) -> p c j i", i=4, j=PACK),
+                out=w5_rounded[b][:].rearrange("p (c i j) -> p c j i", i=4, j=PACK),
                 in_=w5_raw[b][:].rearrange("p j (c i) -> p c j i", i=4),
             )
-        pair_values(6)
+        pair_values(6, freed=4)
         finish_hi(4)
         finish_hi(5)
-        last = 2 * PACK - 1
-        put(6, idx4, h2[6], gate2)
-        put(last, idx4, h2[last], gate2)
-        put(6, idx3, h1[6], gate1)
-        xq_lo = quantize("xq_lo", x_lo[:].rearrange("p c t -> p (c t)"), codes_tile("xq_lo", NP, "gate2_3")[:])
-        fetch_tile(6)
+        put2(6)
+        put2(LAST)
+        put1(6)
+        xq_lo = quantize("xq_lo", x_lo[:].rearrange("p c t -> p (c t)"), sbuf("xq_lo", [P, NP], U32, "gate2_3")[:])
+        fetch(6)
         finish_hi(6)
-        w5q = [quantize("w5q0", w5_grouped[0][:], codes_tile("w5q0", N, "gate1_2")[:])]
-        put(last, idx3, h1[last], gate1)
-        w5q.append(quantize("w5q1", w5_grouped[1][:], codes_tile("w5q1", N, PAGE_SLOT[6])[:]))
+        put1(LAST)
+        w5q = quantize_passes("w5q", w5_rounded, PAGE_TAG[6])
 
         def passes(acc, second, pair, b, xq, c0):
             for u in range(2):
@@ -386,19 +369,16 @@ def tile_list_crock_slot_scores_kernel(
                 if second:
                     lhsT, lhsT_scale = w5q[b][0][:, cols].bitcast(FP8X4), w5q[b][1][:, cols]
                 else:
-                    lhsT, lhsT_scale = w4_w[:, b, 2 * P * n : 2 * P * (n + 1)].bitcast(FP4X4), w4_sc[:, b, cols]
-                nc.tensor.matmul_mx(out=acc[:, u, :], lhsT=lhsT, lhsT_scale=lhsT_scale,
+                    lhsT, lhsT_scale = w4_w[:, b, 2 * P * n : 2 * P * (n + 1)].bitcast(FP4X4), w4_plane[:, b, cols]
+                nc.tensor.matmul_mx(out=acc[:, CH * u : CH * (u + 1)], lhsT=lhsT, lhsT_scale=lhsT_scale,
                                     rhs=xq[0][:, c0 : c0 + CH].bitcast(FP8X4), rhs_scale=xq[1][:, c0 : c0 + CH],
                                     start=(b == 0 and u == 0), stop=(b == 1 and u == 1))
 
-        accs = {}
+        accs, diffs = {}, {}
 
         def open_sum(c, pair, second):
-            acc = bank("acc%d%d%d" % (c, pair, second), 4 * (c % 2) + 2 * pair + second, [P, 2, CH])
-            accs[(c, pair, second)] = acc
-            passes(acc, second, pair, 0, xq_lo, CH * c)
-
-        diffs = {}
+            accs[(c, pair, second)] = bank("acc%d%d%d" % (c, pair, second), 4 * (c % 2) + 2 * pair + second)
+            passes(accs[(c, pair, second)], second, pair, 0, xq_lo, CH * c)
 
         def close_chunk(c, xq):
             for pair in range(2):
@@ -406,18 +386,17 @@ def tile_list_crock_slot_scores_kernel(
                     if c >= 2:
                         open_sum(c, pair, second)
                     passes(accs[(c, pair, second)], second, pair, 1, xq, 0)
-                slot = 2 * (c % 2) + pair
-                size = work_tile("y2abs%d%d" % (c, pair), "size%d" % slot)
-                nc.scalar.activation(size[:], accs[(c, pair, 1)][:].rearrange("p u c -> p (u c)"), ACT.Abs)
-                diff = work_tile("diff%d%d" % (c, pair), "h2_%d" % slot)
-                nc.vector.tensor_tensor(diff[:], accs[(c, pair, 0)][:].rearrange("p u c -> p (u c)"), size[:], ALU.subtract)
-                diffs[(c, pair)] = diff
+                turn = 2 * (c % 2) + pair
+                size = values("y2_size%d%d" % (c, pair), "size%d" % turn)
+                nc.scalar.activation(size[:], accs[(c, pair, 1)][:], ACT.Abs)
+                diffs[(c, pair)] = values("diff%d%d" % (c, pair), "h2_%d" % turn)
+                nc.vector.tensor_tensor(diffs[(c, pair)][:], accs[(c, pair, 0)][:], size[:], ALU.subtract)
 
         def store_chunk(c):
             for pair in range(2):
                 diff = diffs[(c, pair)]
-                result = raw_tile("result%d%d" % (c, pair), [P, S], F32, RESULT_SLOT[(2 * c + pair) % len(RESULT_SLOT)])
-                if 2 * c + pair >= 2 * NCH - ABS_ON_VECTOR:
+                result = values("result%d%d" % (c, pair), RESULT_TAG[2 * c + pair])
+                if c >= 2 and pair == 1:
                     nc.vector.scalar_tensor_tensor(result[:], diff[:], -1.0, diff[:], ALU.mult, ALU.max)
                 else:
                     nc.scalar.activation(result[:], diff[:], ACT.Abs)
@@ -431,16 +410,13 @@ def tile_list_crock_slot_scores_kernel(
                 for second in (1, 0):
                     open_sum(c, pair, second)
         xq_hi = []
-        tail = picked[last - 1]
         for c in range(NCH):
-            cols = slice(CH * (c % 2), CH * (c % 2 + 1))
-            nc.vector.tensor_copy(tail[:, cols], pages[last][:].indirect(idx5[:, CH * c // 16 : CH * (c + 1) // 16]))
-            nc.scalar.activation(tail[:, cols], tail[:, cols], ACT.Tanh)
-            if c in ROUND_ON_VECTOR:
-                nc.vector.tensor_scalar(x_hi[c][:, :, PACK - 1], tail[:, cols], gains[:, 1, PACK - 1 : PACK], None, ALU.mult)
-            else:
-                nc.scalar.activation(x_hi[c][:, :, PACK - 1], tail[:, cols], ACT.Copy, scale=gains[:, 1, PACK - 1 : PACK])
-            xq_hi.append(quantize("xq_hi%d" % c, x_hi[c][:].rearrange("p c t -> p (c t)"), codes_tile("xq_hi%d" % c, CH, "minus%d" % c)[:]))
+            part = picked[LAST - 1][:, CH * (c % 2) : CH * (c % 2 + 1)]
+            nc.vector.tensor_copy(part, pages[LAST][:].indirect(idx5[:, CH * c // 16 : CH * (c + 1) // 16]))
+            nc.scalar.activation(part, part, ACT.Tanh)
+            nc.vector.tensor_scalar(x_hi[c][:, :, PACK - 1], part, gains[:, 1, PACK - 1 : PACK], None, ALU.mult)
+            codes = sbuf("xq_hi%d" % c, [P, CH], U32, "minus%d" % c)
+            xq_hi.append(quantize("xq_hi%d" % c, x_hi[c][:].rearrange("p c t -> p (c t)"), codes[:]))
         for c in range(NCH):
             close_chunk(c, xq_hi[c])
             if c > 0:

from contextlib import ExitStack

import concourse.mybir as mybir
from concourse.masks import make_identity

K, T, K2, TB, S, H, T2, NP, N = 1024, 2048, 512, 1024, 512, 1024, 2048, 1024, 512
FLOPS = 2 * S * H * (K + 2 * K2) + 2 * 2 * H * N * NP

F32 = mybir.dt.float32
BF16 = mybir.dt.bfloat16
I32 = mybir.dt.int32
U32 = mybir.dt.uint32
U16 = mybir.dt.uint16
U8 = mybir.dt.uint8
FP8X4 = mybir.dt.float8_e4m3fn_x4
FP4X4 = mybir.dt.float4_e2m1fn_x4
ACT = mybir.ActivationFunctionType
ALU = mybir.AluOpType

P = 128
PACK = 4
KP = P * PACK
QUADS = 4
LAST = 2 * PACK - 1
CH = 256
NCH = NP // CH

PAGE_TAG = ["page0", "page1", "page2", "page3", "w3_lo", "w1_raw00", "t_words0", "w1_raw10"]
W5_TAG = ["t_words1", "w1_raw01"]
RESULT_TAG = ["w1_raw01", "w1_raw11", "t_words1", "w3_hi", "w1_raw00", "w3_lo", "page1", "page2"]
PICKED_TAG = ["picked0", "picked1", "picked2", "picked0", "picked2", "picked0", "picked1"]


def tile_list_crock_slot_scores_kernel(
    tc, tab_words, tab_scales, tab2_words, tab2_scales, offs, offs2, offs3, offs4, offs5,
    w1, w2_words, w2_scales, w3, wg1, wg2, page0, gain, w4_words, w4_scales, w5, out,
):
    nc = tc.nc
    with ExitStack() as ctx:
        lists = ctx.enter_context(tc.tile_pool(name="lists", bufs=1))
        keep = ctx.enter_context(tc.tile_pool(name="keep", bufs=1))
        ring = ctx.enter_context(tc.tile_pool(name="ring", bufs=3))
        psum = ctx.enter_context(tc.psum_pool(name="psum", bufs=1))

        def sbuf(name, shape, dtype, tag=None):
            return keep.tile(shape, dtype, name=name, tag=tag or name, align_bytes=64)

        def values(name, tag):
            return sbuf(name, [P, S], F32, tag)

        def bank(name, index):
            return psum.tile([P, S], F32, name=name, tag="bank%d" % index)

        def rounded_tile(name):
            return ring.tile([P, PACK * KP], BF16, name=name, tag="rounded", align_bytes=64)

        def load_list(name, src):
            tile = lists.tile(list(src.shape), U16, name=name)
            nc.sync.dma_start(tile[:], src)
            return tile

        def load_bytes(tile_ap, src):
            nc.sync.dma_start(tile_ap.bitcast(I32), src.bitcast(I32))

        def load_rows(name, w, a, c0, tag=None):
            raw = sbuf(name, [P, PACK, KP], F32, tag)
            nc.sync.dma_start(raw[:], w[KP * a : KP * (a + 1), c0 : c0 + KP].rearrange("(p j) c -> p j c", j=PACK))
            return raw

        def load_gate(name, wg, tag):
            rows = values(name, tag)
            nc.sync.dma_start(rows[:], wg)
            return rows

        pages = {}

        def load_page(i):
            b, t = divmod(i, PACK)
            pages[i] = sbuf("page%d" % i, [P, T2], F32, PAGE_TAG[i])
            nc.sync.dma_start(pages[i][:], page0[KP * b : KP * (b + 1), :].rearrange("(p t) c -> t p c", t=PACK)[t])

        t2_plane = sbuf("t2_plane", [P, TB], U8)
        w2_plane = sbuf("w2_plane", [P, H], U8)
        t_plane = sbuf("t_plane", [P, T], U8)
        w4_plane = sbuf("w4_plane", [P, 2, N], U8)
        for plane in (t2_plane, w2_plane, t_plane, w4_plane):
            nc.vector.memset(plane[:].bitcast(I32), 0)

        identity = sbuf("identity", [P, P], F32)
        make_identity(nc, identity[:])

        t2_words = sbuf("t2_words", [P, TB], U32)
        load_bytes(t2_words[:], tab2_words[0].rearrange("p n i -> p (n i)"))
        idx2 = load_list("idx2", offs2)
        wg2_rows = load_gate("wg2_rows", wg2, "h1_0")
        for q in range(QUADS):
            load_bytes(t2_plane[32 * q : 32 * q + 4, :], tab2_scales[0, 4 * q : 4 * q + 4, :])
        w3_lo = load_rows("w3_lo", w3, 0, 0)
        w2_lo = sbuf("w2_lo", [P, 2 * KP], U8)
        load_bytes(w2_lo[:], w2_words[0, :, 0 : 2 * KP])
        for q in range(QUADS):
            load_bytes(w2_plane[32 * q : 32 * q + 4, :], w2_scales[0, 4 * q : 4 * q + 4, :])
        load_page(0)
        idx4 = load_list("idx4", offs4)
        load_page(1)
        load_page(2)
        w1_raw = {(a, 0): load_rows("w1_raw%d0" % a, w1, a, 0) for a in range(2)}
        wg1_rows = load_gate("wg1_rows", wg1, "h1_1")
        idx1 = load_list("idx1", offs)
        t_words = []
        for a in range(2):
            t_words.append(sbuf("t_words%d" % a, [P, T], U32))
            load_bytes(t_words[a][:], tab_words[a].rearrange("p n i -> p (n i)"))
        for q in range(QUADS):
            load_bytes(t_plane[32 * q : 32 * q + 8, :], tab_scales[:, 4 * q : 4 * q + 4, :])
        load_page(3)
        idx3 = load_list("idx3", offs3)

        def round_dealt(copy, raw, name):
            rounded = rounded_tile(name)
            copy(
                out=rounded[:].rearrange("p (t m j) -> p m j t", t=PACK, j=PACK),
                in_=raw[:].rearrange("p j (m t) -> p m j t", t=PACK),
            )
            return rounded

        def quantize(name, src, codes):
            plane = sbuf(name + "_plane", [P, codes.shape[1]], U8)
            nc.vector.quantize_mx(out=codes.bitcast(FP8X4), scales=plane[:], in_=src)
            return codes, plane

        def quantize_passes(name, rounded, tag=None):
            codes = sbuf(name, [P, len(rounded) * KP], U32, tag)
            return [quantize("%s%d" % (name, a), src[:], codes[:, KP * a : KP * (a + 1)]) for a, src in enumerate(rounded)]

        def gather_table(name, window, idx, dtype):
            tile = sbuf(name, [P, S], dtype)
            nc.vector.tensor_copy(tile[:], window[:].indirect(idx[:]))
            return tile

        def stream2_operands(name, w3_rounded, t0, t1):
            count = t1 - t0
            w3q = quantize("w3q_" + name, w3_rounded[:, KP * t0 : KP * t1], sbuf("w3q_" + name, [P, P * count], U32)[:])
            words = sbuf("w2_dealt_" + name, [P, 2 * P * count], U8)
            plane = sbuf("w2_plane_dealt_" + name, [P, P * count], U8)
            nc.vector.tensor_copy(
                out=words[:].rearrange("p (t m e) -> p m t e", t=count, e=2),
                in_=w2_lo[:].rearrange("p (m t e) -> p m t e", t=PACK, e=2)[:, :, t0:t1, :],
            )
            nc.vector.tensor_copy(
                out=plane[:].rearrange("p (t m) -> p m t", t=count),
                in_=w2_plane[:, 0:KP].rearrange("p (m t) -> p m t", t=PACK)[:, :, t0:t1],
            )
            return [
                (w3q[0][:, P * u : P * (u + 1)], w3q[1][:, P * u : P * (u + 1)],
                 words[:, 2 * P * u : 2 * P * (u + 1)], plane[:, P * u : P * (u + 1)])
                for u in range(count)
            ]

        def turn_gate(name, rows):
            turned = bank(name + "_turned", 4)
            for jt in range(S // P):
                nc.tensor.transpose(turned[:, P * jt : P * (jt + 1)], rows[:, P * jt : P * (jt + 1)], identity[:])
            return turned

        def deal_gate(name, turned, t, spread):
            picked_rows = turned[:].rearrange("p (jt q t) -> p jt q t", jt=S // P, t=PACK)[:, :, :, t]
            nc.scalar.activation(
                spread.rearrange("p (jt r q) -> p jt r q", jt=S // P, r=QUADS),
                picked_rows.unsqueeze(2).broadcast_to([P, S // P, QUADS, 32]),
                ACT.Copy,
            )
            back = bank("%s_back%d" % (name, t), 5 + t % 2)
            for jt in range(S // P):
                nc.tensor.transpose(back[:, P * jt : P * (jt + 1)], spread[:, P * jt : P * (jt + 1)], identity[:])
            dealt = sbuf("%s_%d" % (name, t), [P, S], F32)
            nc.scalar.copy(out=dealt[:], in_=back[:])
            return dealt[:]

        def stream2_direct(i, operands):
            w3_codes, w3_plane, w2_codes, w2_dealt_plane = operands
            side = bank("side%d" % i, i % 2)
            nc.tensor.matmul_mx(out=side[:], lhsT=w3_codes.bitcast(FP8X4), lhsT_scale=w3_plane,
                                rhs=v2_words[:].bitcast(FP8X4), rhs_scale=v2_plane[:], start=True, stop=True)
            size = values("size%d" % i, "size%d" % i)
            nc.scalar.activation(size[:], side[:], ACT.Abs)
            base = bank("base%d" % i, (i + 2) % 4)
            nc.tensor.matmul_mx(out=base[:], lhsT=w2_codes.bitcast(FP4X4), lhsT_scale=w2_dealt_plane,
                                rhs=v2_words[:].bitcast(FP8X4), rhs_scale=v2_plane[:], start=True, stop=True)
            result = values("h2_%d" % i, "h2_%d" % i)[:]
            nc.vector.tensor_tensor(result, base[:], size[:], ALU.subtract)
            return result

        def stream2_turned(w3q):
            minus, sizes = [], []
            for jt in range(S // P):
                entries = slice(P * jt, P * (jt + 1))
                base = bank("base_turned%d" % jt, jt)
                nc.tensor.matmul_mx(out=base[:], lhsT=v2_words[:, entries].bitcast(FP8X4), lhsT_scale=v2_plane[:, entries],
                                    rhs=w2_hi[:].bitcast(FP4X4), rhs_scale=w2_plane[:, KP : 2 * KP], start=True, stop=True)
                minus.append(values("minus_base%d" % jt, "minus%d" % jt))
                nc.scalar.activation(
                    minus[jt][:].rearrange("p (t m) -> p t m", t=PACK),
                    base[:].rearrange("p (m t) -> p t m", t=PACK), ACT.Copy, scale=-1.0,
                )
            for jt in range(S // P):
                entries = slice(P * jt, P * (jt + 1))
                side = bank("side_turned%d" % jt, jt)
                nc.tensor.matmul_mx(out=side[:], lhsT=v2_words[:, entries].bitcast(FP8X4), lhsT_scale=v2_plane[:, entries],
                                    rhs=w3q[0].bitcast(FP8X4), rhs_scale=w3q[1][:], start=True, stop=True)
                sizes.append(values("size_turned%d" % jt, "size%d" % jt))
                nc.scalar.activation(sizes[jt][:], side[:], ACT.Abs)
            return list(zip(sizes, minus))

        def stream2_turn_back(i, parts, result):
            cols = slice(P * (i % PACK), P * (i % PACK + 1))
            total = bank("total%d" % i, i % 2)
            for jt in range(S // P):
                for k in range(2):
                    nc.tensor.matmul(total[:, P * jt : P * (jt + 1)], parts[jt][k][:, cols], identity[:],
                                     start=(k == 0), stop=(k == 1), is_transpose=True)
            nc.scalar.activation(result, total[:], ACT.Copy, scale=-1.0)
            return result

        def stream1(i, w1q, result):
            cols = slice(P * (i % PACK), P * (i % PACK + 1))
            pre = bank("pre%d" % i, 4 + i % PACK)
            for a in range(2):
                nc.tensor.matmul_mx(out=pre[:], lhsT=w1q[a][0][:, cols].bitcast(FP8X4), lhsT_scale=w1q[a][1][:, cols],
                                    rhs=v_words[a][:].bitcast(FP8X4), rhs_scale=v_plane[4 * a : P, :],
                                    start=(a == 0), stop=(a == 1))
            nc.scalar.activation(result, pre[:], ACT.Gelu_apprx_tanh)
            return result

        h1, h2 = {}, {}

        def put1(i):
            nc.vector.tensor_tensor(pages[i][:].indirect(idx3[:]), h1[i], gate1[i % PACK], ALU.mult)

        def put2(i):
            nc.vector.tensor_tensor(pages[i][:].indirect(idx4[:]), h2[i], gate2[i % PACK], ALU.mult)

        v2_words = gather_table("v2_words", t2_words, idx2, U32)
        v2_plane = gather_table("v2_plane", t2_plane, idx2, U8)
        w3_rounded = round_dealt(nc.vector.tensor_copy, w3_lo, "w3_rounded_lo")
        operands = stream2_operands("first", w3_rounded, 0, 1) + stream2_operands("rest", w3_rounded, 1, PACK)
        turned = turn_gate("gate2", wg2_rows)
        spread_rest = sbuf("spread_rest", [P, PACK - 1, S], F32, "w2_lo")
        spreads = [values("spread_first", "spread_first")[:]] + [spread_rest[:, u, :] for u in range(PACK - 1)]
        gate2 = []
        for i in range(PACK):
            h2[i] = stream2_direct(i, operands[i])
            gate2.append(deal_gate("gate2", turned, i, spreads[i]))
            if i < PACK - 1:
                put2(i)
        w1q = quantize_passes("w1q_lo", [round_dealt(nc.scalar.copy, w1_raw[(a, 0)], "w1_rounded%d0" % a) for a in range(2)])
        turned = turn_gate("gate1", wg1_rows)
        gate1 = [deal_gate("gate1", turned, t, spreads[t]) for t in range(PACK)]
        v_words = [gather_table("v_words%d" % a, t_words[a], idx1, U32) for a in range(2)]
        v_plane = gather_table("v_plane", t_plane, idx1, U8)
        for i in range(2):
            h1[i] = stream1(i, w1q, values("h1_%d" % i, "h1_%d" % i)[:])
        put2(PACK - 1)

        w3_hi = load_rows("w3_hi", w3, 0, KP)
        w2_hi = sbuf("w2_hi", [P, 2 * KP], U8)
        load_bytes(w2_hi[:], w2_words[0, :, 2 * KP : 4 * KP])
        for a in range(2):
            w1_raw[(a, 1)] = load_rows("w1_raw%d1" % a, w1, a, KP)
        idx5 = load_list("idx5", offs5)
        gains = sbuf("gains", [P, 2, PACK], F32)
        nc.sync.dma_start(gains[:], gain.rearrange("(b p t) -> p b t", p=P, t=PACK))
        for i in range(PACK, LAST):
            load_page(i)
        w4_w = sbuf("w4_w", [P, 2, 2 * N], U8)
        load_bytes(w4_w[:], w4_words.rearrange("a p n -> p a n"))
        for q in range(QUADS):
            load_bytes(w4_plane[32 * q : 32 * q + 4, :, :], w4_scales[:, 4 * q : 4 * q + 4, :].rearrange("a q n -> q a n"))
        w5_raw = [load_rows("w5_raw%d" % b, w5, b, 0, W5_TAG[b]) for b in range(2)]
        load_page(LAST)

        w3_rounded = round_dealt(nc.scalar.copy, w3_hi, "w3_rounded_hi")
        h1_pair = sbuf("h1_pair", [P, 2, S], F32, "w3_hi")
        for i in range(2, PACK):
            h1[i] = stream1(i, w1q, h1_pair[:, i - 2, :])
        for i in range(PACK):
            put1(i)
            if i == 0:
                parts = stream2_turned(quantize("w3q_hi", w3_rounded[:], sbuf("w3q_hi", [P, KP], U32, "h1_0")[:]))
        w1q = quantize_passes("w1q_hi", [round_dealt(nc.scalar.copy, w1_raw[(a, 1)], "w1_rounded%d1" % a) for a in range(2)])

        def pair_values(i, freed):
            first = values("h2_%d" % i, PAGE_TAG[freed])
            both = sbuf("values%d" % i, [P, 2, S], F32, PAGE_TAG[freed + 1])
            h2[i] = stream2_turn_back(i, parts, first[:])
            h2[i + 1] = stream2_turn_back(i + 1, parts, both[:, 0, :])
            h1[i] = stream1(i, w1q, both[:, 1, :])
            h1[i + 1] = stream1(i + 1, w1q, values("h1_%d" % (i + 1), "h1_1")[:])

        picked = {}

        def fetch(i):
            picked[i] = sbuf("picked_from%d" % i, [P, NP], F32, PICKED_TAG[i])
            nc.vector.tensor_copy(picked[i][:], pages[i][:].indirect(idx5[:]))

        def squash(i):
            for c0 in (0, NP // 2):
                half = picked[i][:, c0 : c0 + NP // 2]
                nc.scalar.activation(half, half, ACT.Tanh)

        x_rows = sbuf("x_rows", [P, PACK, NP], BF16)

        def finish_lo(i):
            squash(i)
            for c0 in (0, NP // 2):
                cols = slice(c0, c0 + NP // 2)
                nc.scalar.activation(x_rows[:, i, cols], picked[i][:, cols], ACT.Copy, scale=gains[:, 0, i : i + 1])

        x_hi = [sbuf("x_hi%d" % c, [P, CH, PACK], BF16) for c in range(NCH)]

        def finish_hi(i):
            t = i % PACK
            squash(i)
            for c in range(NCH):
                nc.scalar.activation(x_hi[c][:, :, t], picked[i][:, CH * c : CH * (c + 1)], ACT.Copy, scale=gains[:, 1, t : t + 1])

        for i in range(3):
            fetch(i)
        finish_lo(0)
        fetch(3)
        finish_lo(1)
        pair_values(4, freed=1)
        finish_lo(2)
        finish_lo(3)
        for put in (put2, put1):
            for i in (4, 5):
                put(i)
        fetch(4)
        fetch(5)

        x_lo = sbuf("x_lo", [P, NP, PACK], BF16, PAGE_TAG[0])
        for c in range(NCH):
            nc.scalar.copy(
                out=x_lo[:, CH * c : CH * (c + 1), :].rearrange("p (c i) t -> p c t i", i=8),
                in_=x_rows[:, :, CH * c : CH * (c + 1)].rearrange("p t (c i) -> p c t i", i=8),
            )
        w5_rounded = [rounded_tile("w5_rounded0"), sbuf("w5_rounded1", [P, PACK * N], BF16, "x_rows")]
        for b in range(2):
            nc.scalar.copy(
                out=w5_rounded[b][:].rearrange("p (c i j) -> p c j i", i=4, j=PACK),
                in_=w5_raw[b][:].rearrange("p j (c i) -> p c j i", i=4),
            )
        pair_values(6, freed=4)
        finish_hi(4)
        finish_hi(5)
        put2(6)
        put2(LAST)
        put1(6)
        xq_lo = quantize("xq_lo", x_lo[:].rearrange("p c t -> p (c t)"), sbuf("xq_lo", [P, NP], U32, "gate2_3")[:])
        fetch(6)
        finish_hi(6)
        put1(LAST)
        w5q = quantize_passes("w5q", w5_rounded, PAGE_TAG[6])

        def passes(acc, second, pair, b, xq, c0):
            for u in range(2):
                n = 2 * pair + u
                cols = slice(P * n, P * (n + 1))
                if second:
                    lhsT, lhsT_scale = w5q[b][0][:, cols].bitcast(FP8X4), w5q[b][1][:, cols]
                else:
                    lhsT, lhsT_scale = w4_w[:, b, 2 * P * n : 2 * P * (n + 1)].bitcast(FP4X4), w4_plane[:, b, cols]
                nc.tensor.matmul_mx(out=acc[:, CH * u : CH * (u + 1)], lhsT=lhsT, lhsT_scale=lhsT_scale,
                                    rhs=xq[0][:, c0 : c0 + CH].bitcast(FP8X4), rhs_scale=xq[1][:, c0 : c0 + CH],
                                    start=(b == 0 and u == 0), stop=(b == 1 and u == 1))

        accs, diffs = {}, {}

        def open_sum(c, pair, second):
            accs[(c, pair, second)] = bank("acc%d%d%d" % (c, pair, second), 4 * (c % 2) + 2 * pair + second)
            passes(accs[(c, pair, second)], second, pair, 0, xq_lo, CH * c)

        def close_chunk(c, xq):
            for pair in range(2):
                for second in (1, 0):
                    if c >= 2:
                        open_sum(c, pair, second)
                    passes(accs[(c, pair, second)], second, pair, 1, xq, 0)
                turn = 2 * (c % 2) + pair
                size = values("y2_size%d%d" % (c, pair), "size%d" % turn)
                nc.scalar.activation(size[:], accs[(c, pair, 1)][:], ACT.Abs)
                diffs[(c, pair)] = values("diff%d%d" % (c, pair), "h2_%d" % turn)
                nc.vector.tensor_tensor(diffs[(c, pair)][:], accs[(c, pair, 0)][:], size[:], ALU.subtract)

        def store_chunk(c):
            for pair in range(2):
                diff = diffs[(c, pair)]
                result = values("result%d%d" % (c, pair), RESULT_TAG[2 * c + pair])
                if c >= 2 and pair == 1:
                    nc.vector.scalar_tensor_tensor(result[:], diff[:], -1.0, diff[:], ALU.mult, ALU.max)
                else:
                    nc.scalar.activation(result[:], diff[:], ACT.Abs)
                nc.sync.dma_start(
                    out[2 * P * pair : 2 * P * (pair + 1), CH * c : CH * (c + 1)].rearrange("(u p) c -> p u c", p=P),
                    result[:].rearrange("p (u c) -> p u c", u=2),
                )

        for c in range(2):
            for pair in range(2):
                for second in (1, 0):
                    open_sum(c, pair, second)
        xq_hi = []
        for c in range(NCH):
            part = picked[LAST - 1][:, CH * (c % 2) : CH * (c % 2 + 1)]
            nc.vector.tensor_copy(part, pages[LAST][:].indirect(idx5[:, CH * c // 16 : CH * (c + 1) // 16]))
            nc.scalar.activation(part, part, ACT.Tanh)
            nc.vector.tensor_scalar(x_hi[c][:, :, PACK - 1], part, gains[:, 1, PACK - 1 : PACK], None, ALU.mult)
            codes = sbuf("xq_hi%d" % c, [P, CH], U32, "minus%d" % c)
            xq_hi.append(quantize("xq_hi%d" % c, x_hi[c][:].rearrange("p c t -> p (c t)"), codes[:]))
        for c in range(NCH):
            close_chunk(c, xq_hi[c])
            if c > 0:
                store_chunk(c - 1)
        store_chunk(NCH - 1)
